import numpy as np
import ml_dtypes


def mxq(x, axis, fmt="e4m3"):
    dtype, down = {"e4m3": (ml_dtypes.float8_e4m3fn, 7), "e5m2": (ml_dtypes.float8_e5m2, 14)}[fmt]
    v = np.moveaxis(np.asarray(x, np.float32).astype(ml_dtypes.bfloat16).astype(np.float64), axis, -1)
    blocks = v.reshape(v.shape[:-1] + (-1, 32))
    amax = np.abs(blocks).max(-1, keepdims=True)
    byte = np.maximum(np.where(amax > 0, np.frexp(amax)[1] - 1 + 127, 0) - down, 1)
    scale = np.exp2(byte - 127.0)
    codes = (blocks / scale).astype(np.float32).astype(dtype).astype(np.float64)
    return np.moveaxis((codes * scale).reshape(v.shape), -1, axis)


WIDE = False


def mx_kscale(k):
    if not WIDE:
        return np.ones(k)
    levels = np.array([10, -10, 5, -5, 0])
    if k % 512:
        return np.exp2(np.random.permutation(np.resize(levels, k // 32))).repeat(32)
    a = np.empty((k // 512, 16))
    for p in range(k // 512):
        a[p, :8] = np.random.permutation(np.resize(levels, 8))
        for g in range(8):
            far = levels[np.abs(levels - a[p, g]) >= 10]
            a[p, g + 8] = far[np.random.randint(len(far))]
    return np.exp2(a.ravel()).repeat(32)


def f64(x):
    return np.asarray(x).astype(np.float64)


def striped(idx):
    return np.tile(idx.reshape(-1, 16).T, (8, 1)).astype(np.uint16)


def unstriped(offs):
    return offs[:16].T.reshape(-1).astype(np.int64)


E2M1 = np.array([0.0, 0.5, 1.0, 1.5, 2.0, 3.0, 4.0, 6.0, -0.0, -0.5, -1.0, -1.5, -2.0, -3.0, -4.0, -6.0])


def pack_weight(w, fmt):
    k, n = w.shape
    w = f64(np.asarray(w, np.float32).astype(ml_dtypes.bfloat16)).reshape(k // 32, 32, n)
    amax = np.abs(w).max(1)
    if fmt == "e4m3":
        byte = np.frexp(amax)[1] - 1 + 127 - 7
    else:
        mant, ex = np.frexp(amax / 6.0)
        byte = np.where(mant > 0.5, ex, ex - 1) + 127
    byte = np.clip(np.where(amax > 0, byte, 1), 1, 254)
    scaled = (w * np.exp2(127.0 - byte)[:, None, :]).reshape(k, n).astype(np.float32)
    by_word = np.ascontiguousarray(scaled.reshape(k // 512, 128, 4, n).transpose(0, 1, 3, 2))
    if fmt == "e4m3":
        words = by_word.astype(ml_dtypes.float8_e4m3fn).view(np.uint8)
    else:
        c = by_word.astype(ml_dtypes.float4_e2m1fn).view(np.uint8) & 0xF
        words = (c[..., 0::2] | (c[..., 1::2] << 4)).reshape(k // 512, 128, 2 * n)
    return np.ascontiguousarray(words), np.ascontiguousarray(byte.astype(np.uint8).reshape(k // 512, 16, n))


def unpack_weight(words, scales, fmt):
    g, _, n = scales.shape
    words = np.ascontiguousarray(words).reshape(g, 128, n, -1)
    if fmt == "e4m3":
        vals = words.view(ml_dtypes.float8_e4m3fn).astype(np.float64)
    else:
        nib = np.empty((g, 128, n, 4), np.uint8)
        nib[..., 0::2] = words & 0xF
        nib[..., 1::2] = words >> 4
        vals = E2M1[nib]
    vals = vals * np.repeat(np.exp2(scales.astype(np.float64) - 127.0), 8, axis=1)[..., None]
    return vals.transpose(0, 1, 3, 2).reshape(g * 512, n)


def gelu(v):
    return 0.5 * v * (1.0 + np.tanh(np.sqrt(2.0 / np.pi) * (v + 0.044715 * v**3)))


K, T, S, P, H, N, T2 = 1536, 2048, 512, 512, 1024, 640, 1024


def setup_inputs():
    n = np.random.standard_normal
    s = mx_kscale(K)[:, None]
    u = mx_kscale(H)[:, None]
    d = {}
    d["tab_words"], d["tab_scales"] = pack_weight(n((K, T)) * s, "e4m3")
    d["offs"] = striped(np.random.permutation(T)[:S])
    d["offs2"] = striped(np.random.permutation(T2)[:S])
    d["offs3"] = striped(np.random.permutation(T2)[:P])
    d["offs4"] = striped(np.random.permutation(T2)[:P])
    d["w1"] = (n((K, H)) / s / K ** 0.5).astype(np.float32)
    d["w2_words"], d["w2_scales"] = pack_weight(n((K, H)) / s / K ** 0.5, "e2m1")
    d["gain1"] = (np.exp(0.3 * n(H)) * u[:, 0]).astype(np.float32)
    d["page0"] = (n((H, T2)) * u).astype(np.float32)
    d["wgs"] = np.exp(0.3 * n((128, S))).astype(np.float32)
    d["w3"] = (n((H, H)) / u / H ** 0.5).astype(np.float32)
    d["gain2"] = (1.5 * np.exp(0.3 * n(H)) * u[:, 0]).astype(np.float32)
    d["w4_words"], d["w4_scales"] = pack_weight(n((H, N)) / u / H ** 0.5, "e4m3")
    d["page1"] = n((N, T2)).astype(np.float32)
    d["wgo"] = np.exp(0.3 * n((128, P))).astype(np.float32)
    return d


def reference(tab_words, tab_scales, offs, offs2, offs3, offs4, w1, w2_words, w2_scales, gain1,
              page0, wgs, w3, gain2, w4_words, w4_scales, page1, wgo):
    v = unpack_weight(tab_words, tab_scales, "e4m3")[:, unstriped(offs)]
    a = mxq(f64(w1), 0, "e4m3").T @ v
    b = unpack_weight(w2_words, w2_scales, "e2m1").T @ v
    h = f64(gain1)[:, None] * (a + np.abs(b))
    page = f64(page0).copy()
    page[:, unstriped(offs2)] = np.tile(f64(wgs), (H // 128, 1)) * h
    x = page[:, unstriped(offs3)]
    e = mxq(f64(w3), 0, "e4m3").T @ mxq(x, 0, "e4m3")
    z = x + f64(gain2)[:, None] * np.tanh(e)
    y = unpack_weight(w4_words, w4_scales, "e4m3").T @ mxq(z, 0, "e4m3")
    out = f64(page1).copy()
    out[:, unstriped(offs4)] = np.tile(f64(wgo), (N // 128, 1)) * y
    return out

@@ -1,0 +1,403 @@
+from contextlib import ExitStack
+
+import concourse.mybir as mybir
+from concourse.masks import make_identity
+
+K, T, S, H, N, T2 = 1536, 2048, 512, 1024, 640, 1024
+FLOPS = 2 * S * (2 * K * H + H * H + H * N)
+
+F32 = mybir.dt.float32
+BF16 = mybir.dt.bfloat16
+I32 = mybir.dt.int32
+U32 = mybir.dt.uint32
+U16 = mybir.dt.uint16
+U8 = mybir.dt.uint8
+FP8X4 = mybir.dt.float8_e4m3fn_x4
+FP4X4 = mybir.dt.float4_e2m1fn_x4
+ACT = mybir.ActivationFunctionType
+MULT = mybir.AluOpType.mult
+ADD = mybir.AluOpType.add
+
+P = 128
+PACK = 4
+BLOCK = P * PACK
+KP = K // BLOCK
+HB = H // BLOCK
+NT = N // P
+CH = S // P
+HALF = S // 2
+LCOL = HALF // 16
+
+
+def tile_list_truffle_survey_walk_kernel(
+    tc, tab_words, tab_scales, offs, offs2, offs3, offs4, w1, w2_words, w2_scales, gain1,
+    page0, wgs, w3, gain2, w4_words, w4_scales, page1, wgo, out,
+):
+    nc = tc.nc
+    with ExitStack() as ctx:
+        sb = ctx.enter_context(tc.tile_pool(name="sb", bufs=1))
+        ps = ctx.enter_context(tc.psum_pool(name="ps", bufs=1))
+
+        def sbuf(name, shape, dtype, slot=None):
+            return sb.tile([P] + shape, dtype, name=name, tag=slot or name, align_bytes=64)
+
+        def bank(name, slot):
+            return ps.tile([P, BLOCK], F32, name=name, tag=slot)
+
+        def load_scales(name, src, passes, width, queue):
+            plane = sbuf(name, [passes, width], U8)
+            flat = plane[:].rearrange("p a c -> p (a c)").bitcast(I32)
+            cut = flat.shape[1] // 2
+            nc.gpsimd.memset(flat[:, :cut], 0)
+            nc.vector.memset(flat[:, cut:], 0)
+            rows = src.rearrange("a (Q r) c -> r Q a c", r=4)
+            for r in range(4):
+                queue.dma_start(out=plane[r:P:32].bitcast(I32), in_=rows[r].bitcast(I32))
+            return plane
+
+        def load_list(name, src):
+            lst = sbuf(name, [S // 16], U16)
+            nc.sync.dma_start(lst[:], src)
+            return lst
+
+        def load_rows(name, src, a, b, slot):
+            raw = sbuf(name, [PACK, BLOCK], F32, slot)
+            nc.sync.dma_start(
+                out=raw[:],
+                in_=src[a * BLOCK : (a + 1) * BLOCK, b * BLOCK : (b + 1) * BLOCK].rearrange("(p t) c -> p t c", t=PACK),
+            )
+            return raw
+
+        def load_page(s):
+            b, t = divmod(s, PACK)
+            tile = sbuf("page%d" % s, [T2], F32)
+            nc.sync.dma_start(out=tile[:], in_=page0[b * BLOCK : (b + 1) * BLOCK, :].rearrange("(p t) c -> t p c", t=PACK)[t])
+            return tile
+
+        def weave(copy, name, src, slot):
+            width = src.shape[2]
+            woven = sbuf(name, [width * PACK], BF16, slot) if isinstance(slot, str) else slot
+            copy(woven[:].rearrange("p (c i t) -> p c t i", i=4, t=PACK), src[:].rearrange("p t (c i) -> p c t i", i=4))
+            return woven
+
+        def weave_dealt(name, src, slot):
+            woven = sbuf(name, [BLOCK * PACK], BF16, slot) if isinstance(slot, str) else slot
+            nc.scalar.copy(
+                woven[:].rearrange("p (u q t) -> p q t u", u=PACK, t=PACK), src[:].rearrange("p t (q u) -> p q t u", u=PACK)
+            )
+            return woven
+
+        def quantize(name, woven):
+            width = woven.shape[1] // PACK
+            codes = sbuf(name + "_codes", [width], U32)
+            scales = sbuf(name + "_scales", [width], U8)
+            nc.vector.quantize_mx(out=codes[:].bitcast(FP8X4), scales=scales[:], in_=woven[:])
+            return codes, scales
+
+        def dealt_view(acc):
+            return acc[:].rearrange("p (q t) -> p t q", t=PACK)
+
+        tab = []
+        for a in range(KP):
+            words = sbuf("tab%d" % a, [T], I32, "R%d" % a)
+            tab.append(words)
+
+        def load_tab(a):
+            nc.sync.dma_start(out=tab[a][:], in_=tab_words[a].rearrange("p n t -> p (n t)").bitcast(I32))
+
+        def load_w2(b):
+            words = sbuf("w2w%d" % b, [KP, 2 * BLOCK], U8)
+            nc.sync.dma_start(
+                out=words[:].bitcast(I32),
+                in_=w2_words.rearrange("a p c -> p a c")[:, :, 2 * BLOCK * b : 2 * BLOCK * (b + 1)].bitcast(I32),
+            )
+            return words
+
+        idx = load_list("idx", offs)
+        wgs_rows = sbuf("wgs_rows", [S], F32)
+        nc.sync.dma_start(out=wgs_rows[:], in_=wgs)
+        load_tab(0)
+        tab_plane = load_scales("tab_plane", tab_scales, KP, T, nc.sync)
+        load_tab(1)
+        load_tab(2)
+        w2_plane = load_scales("w2_plane", w2_scales, KP, H, nc.sync)
+        w2w = [load_w2(0)]
+        w1raw = {(0, 0): load_rows("w1raw00", w1, 0, 0, "R3")}
+        w1raw[1, 0] = load_rows("w1raw10", w1, 1, 0, "R4")
+        last_raw = []
+        for u, slot in enumerate(("R5", "X0")):
+            raw = sbuf("w1last%d" % u, [PACK, HALF], F32, slot)
+            nc.sync.dma_start(
+                out=raw[:], in_=w1[2 * BLOCK :, u * HALF : (u + 1) * HALF].rearrange("(p t) c -> p t c", t=PACK)
+            )
+            last_raw.append(raw)
+        ident = sbuf("ident", [P], F32)
+        make_identity(nc, ident[:])
+
+        vw, vs = [], []
+        for a in range(KP):
+            words = sbuf("vw%d" % a, [S], U32)
+            nc.vector.tensor_copy(words[:], tab[a][:].bitcast(U32).indirect(idx[:]))
+            scales = sbuf("vs%d" % a, [S], U8)
+            nc.vector.tensor_copy(scales[:], tab_plane[:, a, :].indirect(idx[:]))
+            vw.append(words)
+            vs.append(scales)
+
+        pages = {}
+        w3raw = {}
+        idx2 = load_list("idx2", offs2)
+        g1 = sbuf("g1", [HB, PACK], F32)
+        nc.sync.dma_start(out=g1[:], in_=gain1.rearrange("(b p t) -> p b t", b=HB, t=PACK))
+        pages[0] = load_page(0)
+        idx3 = load_list("idx3", offs3)
+        w2w.append(load_w2(1))
+        w1raw[0, 1] = load_rows("w1raw01", w1, 0, 1, "R0")
+        pages[1] = load_page(1)
+        w1raw[1, 1] = load_rows("w1raw11", w1, 1, 1, "R1")
+        w1raw[2, 1] = load_rows("w1raw21", w1, 2, 1, "R2")
+        pages[2] = load_page(2)
+        pages[3] = load_page(3)
+
+        turned = bank("wgs_turned", "ab0")
+        for c in range(CH):
+            nc.tensor.transpose(turned[:, c * P : (c + 1) * P], wgs_rows[:, c * P : (c + 1) * P], ident[:])
+        spread = []
+        spread_all = sbuf("spread", [CH, PACK, 4, 32], F32, "AA")
+        for c in range(CH):
+            tile = spread_all[:, c]
+            nc.scalar.copy(
+                tile[:],
+                turned[:, c * P : (c + 1) * P].rearrange("p (q t) -> p t q", t=PACK).unsqueeze(2).to_broadcast([P, PACK, 4, 32]),
+            )
+            spread.append(tile)
+        wg = sbuf("wg", [PACK, S], F32)
+        for t in range(PACK):
+            acc = bank("wg_bank%d" % t, "hh%d" % t)
+            for c in range(CH):
+                nc.tensor.transpose(acc[:, c * P : (c + 1) * P], spread[c][:, t].rearrange("p r q -> p (r q)"), ident[:])
+            nc.scalar.copy(wg[:, t, :], acc[:])
+
+        def add_turned(acc, src, t, c, start, stop):
+            nc.tensor.matmul(acc[:, c * P : (c + 1) * P], src[:, t, :], ident[:], start=start, stop=stop, is_transpose=True)
+
+        def abs_product(b, banks):
+            mags = []
+            for c in range(CH):
+                acc = bank("bT%d%d" % (b, c), banks % c)
+                cols = slice(c * P, (c + 1) * P)
+                for a in range(KP):
+                    nc.tensor.matmul_mx(
+                        out=acc[:], lhsT=vw[a][:, cols].bitcast(FP8X4), lhsT_scale=vs[a][:, cols],
+                        rhs=w2w[b][:, a, :].bitcast(FP4X4), rhs_scale=w2_plane[:, a, b * BLOCK : (b + 1) * BLOCK],
+                        start=(a == 0), stop=(a == KP - 1),
+                    )
+                mag = sbuf("mag%d%d" % (b, c), [PACK, P], F32, "B%d" % c)
+                nc.scalar.activation(mag[:], dealt_view(acc), ACT.Abs)
+                mags.append(mag)
+            return mags
+
+        def open_sums(b, mags):
+            sums = [bank("hsum%d%d" % (b, t), "hh%d" % t) for t in range(PACK)]
+            for t in range(PACK):
+                for c in range(CH):
+                    add_turned(sums[t], mags[c], t, c, c == 0, False)
+            return sums
+
+        def w1_pass(accs, a, quantised, first=0):
+            codes, scales = quantised
+            end = first + codes.shape[1]
+            for c in range(CH):
+                cols = slice(c * P, (c + 1) * P)
+                nc.tensor.matmul_mx(
+                    out=accs[c][:, first:end], lhsT=vw[a][:, cols].bitcast(FP8X4), lhsT_scale=vs[a][:, cols],
+                    rhs=codes[:].bitcast(FP8X4), rhs_scale=scales[:],
+                    start=(a == 0), stop=(a == KP - 1 and end == BLOCK),
+                )
+
+        def linear_part(b, accs, sums, copies):
+            first = sbuf("linfirst%d" % b, [CH, 1, P], F32, "AA")
+            for c in range(CH):
+                copies[c % 2](first[:, c, 0], dealt_view(accs[c])[:, 0])
+            for c in range(CH):
+                add_turned(sums[0], first[:, c], 0, c, False, c == CH - 1)
+            hs = [state(b, 0, sums)]
+            lin = sbuf("lin%d" % b, [CH, PACK, P], F32, "AA")
+            for c in range(CH):
+                nc.scalar.copy(lin[:, c, 1:], dealt_view(accs[c])[:, 1:])
+            for t in range(1, PACK):
+                for c in range(CH):
+                    add_turned(sums[t], lin[:, c], t, c, False, c == CH - 1)
+            return hs
+
+        def state(b, t, sums, h=None):
+            if h is None:
+                h = sbuf("h%d%d" % (b, t), [S], F32, "h%d" % ((PACK * b + t) % 6))
+            nc.scalar.activation(h[:], sums[t][:], ACT.Copy, scale=g1[:, b, t : t + 1])
+            return h
+
+        def put(s, h):
+            nc.vector.tensor_tensor(pages[s][:].indirect(idx2[:]), h[:], wg[:, s % PACK, :], MULT)
+
+        def recall(s, half, x):
+            nc.vector.tensor_copy(x[:, s % PACK, :], pages[s][:].indirect(idx3[:, half * LCOL : (half + 1) * LCOL]))
+
+        accs = [bank("aT0%d" % c, "ab%d" % c) for c in range(CH)]
+        for a in range(KP - 1):
+            woven = weave(nc.vector.tensor_copy, "w1wv%d0" % a, w1raw[a, 0], "H%d" % a)
+            w1_pass(accs, a, quantize("w1q%d0" % a, woven))
+        for u in range(2):
+            woven = weave((nc.scalar.copy, nc.vector.tensor_copy)[u], "w1lastwv%d" % u, last_raw[u], "h%d" % (4 + u))
+            w1_pass(accs, KP - 1, quantize("w1lastq%d" % u, woven), u * HALF)
+        sums = open_sums(0, abs_product(0, "hh%d"))
+        hs = linear_part(0, accs, sums, (nc.scalar.copy, nc.vector.tensor_copy))
+        hs.append(state(0, 1, sums))
+
+        w3raw[0, 0] = load_rows("w3raw00", w3, 0, 0, "R3")
+        w3raw[1, 0] = load_rows("w3raw10", w3, 1, 0, "R4")
+        pages[4] = load_page(4)
+        pages[5] = load_page(5)
+        w3raw[0, 1] = load_rows("w3raw01", w3, 0, 1, "R5")
+        pages[6] = load_page(6)
+
+        x = {}
+        x[0, 0] = sbuf("x00", [PACK, HALF], F32, "H0")
+        pair = sbuf("w1wv_pair", [2, BLOCK * PACK], BF16, "AA")
+        wovens = [weave(nc.scalar.copy, "", w1raw[a, 1], pair[:, a]) for a in range(2)]
+        hs.append(state(0, 2, sums, sbuf("h02", [S], F32, "R1")))
+        mags = abs_product(1, "ab%d")
+        wovens.append(weave(nc.scalar.copy, "w1wv21", w1raw[2, 1], "AB"))
+        late = sbuf("h0late", [S], F32, "R2")
+        hs.append(state(0, 3, sums, late))
+        sums = open_sums(1, mags)
+        accs = [bank("aT1%d" % c, "ab%d" % c) for c in range(CH)]
+        for t in range(PACK):
+            for a in ((), (), (0, 1), (2,))[t]:
+                w1_pass(accs, a, quantize("w1q%d1" % a, wovens[a]))
+            put(t, hs[t])
+            recall(t, 0, x[0, 0])
+
+        w3raw[1, 1] = load_rows("w3raw11", w3, 1, 1, "R0")
+        pages[7] = load_page(7)
+        g2 = sbuf("g2", [HB, PACK], F32)
+        nc.sync.dma_start(out=g2[:], in_=gain2.rearrange("(b p t) -> p b t", b=HB, t=PACK))
+        idx4 = load_list("idx4", offs4)
+        w4_plane = load_scales("w4_plane", w4_scales, HB, N, nc.sync)
+        w4w = sbuf("w4w", [HB, N], I32)
+        nc.sync.dma_start(out=w4w[:], in_=w4_words.rearrange("a p n t -> p a (n t)").bitcast(I32))
+        wo = sbuf("wo", [S], F32)
+        nc.sync.dma_start(out=wo[:], in_=wgo)
+        walk = []
+        for n in range(NT):
+            tile = sbuf("walk%d" % n, [T2], F32)
+            nc.sync.dma_start(out=tile[:], in_=page1[n * P : (n + 1) * P, :])
+            walk.append(tile)
+
+        hs = linear_part(1, accs, sums, (nc.scalar.copy, nc.scalar.copy))
+        hs.extend(state(1, t, sums) for t in range(1, PACK))
+        x[1, 0] = sbuf("x10", [PACK, HALF], F32, "H1")
+        xq = {}
+        w3wv = {}
+        put(4, hs[0])
+        recall(4, 0, x[1, 0])
+        pair = sbuf("w3wv_pair", [2, BLOCK * PACK], BF16, "AA")
+        for a in range(HB):
+            w3wv[a, 0] = weave_dealt("", w3raw[a, 0], pair[:, a])
+        for t in range(1, PACK):
+            put(PACK + t, hs[t])
+            recall(PACK + t, 0, x[1, 0])
+            if t == 1:
+                xq[0, 0] = quantize("xq00", weave(nc.scalar.copy, "xwv00", x[0, 0], "h5"))
+            if t == 2:
+                w3wv[1, 1] = weave_dealt("w3wv11", w3raw[1, 1], "AB")
+                w3wv[0, 1] = weave_dealt("w3wv01", w3raw[0, 1], "h0")
+        xwv10 = weave(nc.scalar.copy, "xwv10", x[1, 0], "X0")
+        w3q = {key: quantize("w3q%d%d" % key, w3wv[key]) for key in w3wv}
+        xq[1, 0] = quantize("xq10", xwv10)
+
+        def stage2(half, k):
+            b, pair = divmod(k, 2)
+            acc = bank("e%d%d" % (half, k), "ab%d" % k)
+            for u in range(2):
+                cols = slice((2 * pair + u) * P, (2 * pair + u + 1) * P)
+                for a in range(HB):
+                    nc.tensor.matmul_mx(
+                        out=acc[:, u * HALF : (u + 1) * HALF],
+                        lhsT=w3q[a, b][0][:, cols].bitcast(FP8X4), lhsT_scale=w3q[a, b][1][:, cols],
+                        rhs=xq[a, half][0][:].bitcast(FP8X4), rhs_scale=xq[a, half][1][:],
+                        start=(a == 0), stop=(a == HB - 1),
+                    )
+            th = sbuf("tanh%d%d" % (half, k), [2, HALF], F32, "B%d" % k)
+            nc.scalar.activation(th[:].rearrange("p u j -> p (u j)"), acc[:], ACT.Tanh)
+            return th
+
+        def combine(half, k, th, z):
+            b, pair = divmod(k, 2)
+            for u in range(2):
+                t = 2 * pair + u
+                nc.vector.scalar_tensor_tensor(z[:, t, :], th[:, u, :], g2[:, b, t : t + 1], x[b, half][:, t, :], MULT, ADD)
+
+        zq = {}
+
+        def stage3(half, n, bank_slot):
+            acc = bank("y%d%d" % (half, n), bank_slot)
+            cols = slice(n * P, (n + 1) * P)
+            for a in range(HB):
+                nc.tensor.matmul_mx(
+                    out=acc[:, :HALF], lhsT=w4w[:, a, cols].bitcast(FP8X4), lhsT_scale=w4_plane[:, a, cols],
+                    rhs=zq[a, half][0][:].bitcast(FP8X4), rhs_scale=zq[a, half][1][:],
+                    start=(a == 0), stop=(a == HB - 1),
+                )
+            return acc
+
+        def leave(half, n, acc, slot):
+            y = sbuf("ysb%d%d" % (half, n), [HALF], F32, slot)
+            nc.scalar.copy(y[:], acc[:, :HALF])
+            return y
+
+        def place(half, n, y):
+            nc.vector.tensor_tensor(
+                walk[n][:].indirect(idx4[:, half * LCOL : (half + 1) * LCOL]), y[:], wo[:, half * HALF : (half + 1) * HALF], MULT
+            )
+
+        ths = [stage2(0, k) for k in range(4)]
+        x[0, 1] = sbuf("x01", [PACK, HALF], F32, "X0")
+        for t in range(PACK):
+            recall(t, 1, x[0, 1])
+        z0 = sbuf("z00", [PACK, HALF], BF16, "h2")
+        z1 = sbuf("z10", [PACK, HALF], BF16, "h3")
+        combine(0, 0, ths[0], z0)
+        combine(0, 1, ths[1], z0)
+        zwv0 = weave(nc.scalar.copy, "zwv00", z0, "h4")
+        combine(0, 2, ths[2], z1)
+        combine(0, 3, ths[3], z1)
+        zwv1 = weave(nc.scalar.copy, "zwv10", z1, "h5")
+        zq[0, 0] = quantize("zq00", zwv0)
+        x[1, 1] = sbuf("x11", [PACK, HALF], F32, "H1")
+        for t in range(PACK):
+            recall(PACK + t, 1, x[1, 1])
+        zq[1, 0] = quantize("zq10", zwv1)
+        xq[0, 1] = quantize("xq01", weave(nc.scalar.copy, "xwv01", x[0, 1], "h3"))
+        yacc = [stage3(0, n, "hh%d" % n) for n in range(4)]
+        place(0, 0, leave(0, 0, yacc[0], "Y0"))
+        yacc.append(stage3(0, 4, "hh0"))
+        place(0, 1, leave(0, 1, yacc[1], "Y1"))
+        xq[1, 1] = quantize("xq11", weave(nc.scalar.copy, "xwv11", x[1, 1], "h0"))
+        place(0, 2, leave(0, 2, yacc[2], "Y2"))
+        ths = [stage2(1, k) for k in range(4)]
+        z0 = sbuf("z01", [PACK, HALF], BF16, "h1")
+        z1 = sbuf("z11", [PACK, HALF], BF16, "h2")
+        combine(1, 0, ths[0], z0)
+        combine(1, 1, ths[1], z0)
+        combine(1, 2, ths[2], z1)
+        y3 = leave(0, 3, yacc[3], "B2")
+        combine(1, 3, ths[3], z1)
+        zwv0 = weave(nc.scalar.copy, "zwv01", z0, "h4")
+        zwv1 = weave(nc.scalar.copy, "zwv11", z1, "h5")
+        place(0, 3, y3)
+        zq[0, 1] = quantize("zq01", zwv0)
+        zq[1, 1] = quantize("zq11", zwv1)
+        place(0, 4, leave(0, 4, yacc[4], "h2"))
+        for n in range(NT):
+            acc = stage3(1, n, "hh%d" % ((n + 1) % 4))
+            place(1, n, leave(1, n, acc, ("Y0", "Y1", "Y2", "B0", "B1")[n]))
+            nc.sync.dma_start(out=out[n * P : (n + 1) * P, :], in_=walk[n][:])

@@ -87,10 +87,11 @@ def tile_list_truffle_survey_walk_kernel(
             )
             return woven
 
-        def quantize(name, woven):
+        def quantize(name, woven, scales=None):
             width = woven.shape[1] // PACK
             codes = sbuf(name + "_codes", [width], U32)
-            scales = sbuf(name + "_scales", [width], U8)
+            if scales is None:
+                scales = sbuf(name + "_scales", [width], U8)
             nc.vector.quantize_mx(out=codes[:].bitcast(FP8X4), scales=scales[:], in_=woven[:])
             return codes, scales
 
@@ -113,24 +114,40 @@ def tile_list_truffle_survey_walk_kernel(
             )
             return words
 
+        def load_w1_columns(name, a, first, width, slot):
+            raw = sbuf(name, [PACK, width], F32, slot) if isinstance(slot, str) else slot
+            nc.sync.dma_start(
+                out=raw[:], in_=w1[a * BLOCK : (a + 1) * BLOCK, first : first + width].rearrange("(p t) c -> p t c", t=PACK)
+            )
+            return raw
+
+        def load_w2_columns(name, first, width):
+            words = sbuf(name, [KP, 2 * width], U8)
+            nc.sync.dma_start(
+                out=words[:].bitcast(I32),
+                in_=w2_words.rearrange("a p c -> p a c")[:, :, 2 * first : 2 * (first + width)].bitcast(I32),
+            )
+            return words
+
+        def load_plain_page(s):
+            tile = sbuf("page%d" % s, [T2], F32)
+            nc.sync.dma_start(out=tile[:], in_=page0[s * P : (s + 1) * P, :])
+            return tile
+
         idx = load_list("idx", offs)
         wgs_rows = sbuf("wgs_rows", [S], F32)
         nc.sync.dma_start(out=wgs_rows[:], in_=wgs)
-        load_tab(0)
+        g1rows = sbuf("g1rows", [PACK], F32)
+        with nc.allow_non_contiguous_dma(reason="one gain for each partition and slice"):
+            nc.sync.dma_start(out=g1rows[:], in_=gain1[:BLOCK].rearrange("(s p) -> p s", p=P))
         tab_plane = load_scales("tab_plane", tab_scales, KP, T, nc.sync)
+        load_tab(0)
         load_tab(1)
+        w2_planes = [load_scales("w2_plane0", w2_scales[:, :, :BLOCK], KP, BLOCK, nc.sync)]
         load_tab(2)
-        w2_plane = load_scales("w2_plane", w2_scales, KP, H, nc.sync)
-        w2w = [load_w2(0)]
-        w1raw = {(0, 0): load_rows("w1raw00", w1, 0, 0, "R3")}
-        w1raw[1, 0] = load_rows("w1raw10", w1, 1, 0, "R4")
-        last_raw = []
-        for u, slot in enumerate(("R5", "X0")):
-            raw = sbuf("w1last%d" % u, [PACK, HALF], F32, slot)
-            nc.sync.dma_start(
-                out=raw[:], in_=w1[2 * BLOCK :, u * HALF : (u + 1) * HALF].rearrange("(p t) c -> p t c", t=PACK)
-            )
-            last_raw.append(raw)
+        w2first = load_w2_columns("w2first", 0, P)
+        raw_all = sbuf("w1s0raw", [KP, PACK, P], F32, "R3")
+        raw0 = [load_w1_columns("", a, 0, P, raw_all[:, a]) for a in range(KP)]
         ident = sbuf("ident", [P], F32)
         make_identity(nc, ident[:])
 
@@ -145,20 +162,32 @@ def tile_list_truffle_survey_walk_kernel(
 
         pages = {}
         w3raw = {}
+        w1raw = {}
         idx2 = load_list("idx2", offs2)
-        g1 = sbuf("g1", [HB, PACK], F32)
-        nc.sync.dma_start(out=g1[:], in_=gain1.rearrange("(b p t) -> p b t", b=HB, t=PACK))
-        pages[0] = load_page(0)
+        pages[0] = load_plain_page(0)
+        w2rest = load_w2_columns("w2rest", P, BLOCK - P)
+        raw_all = sbuf("w1s1raw", [KP, PACK, P], F32, "R4")
+        raw1 = [load_w1_columns("", a, P, P, raw_all[:, a]) for a in range(KP)]
         idx3 = load_list("idx3", offs3)
-        w2w.append(load_w2(1))
-        w1raw[0, 1] = load_rows("w1raw01", w1, 0, 1, "R0")
-        pages[1] = load_page(1)
-        w1raw[1, 1] = load_rows("w1raw11", w1, 1, 1, "R1")
-        w1raw[2, 1] = load_rows("w1raw21", w1, 2, 1, "R2")
-        pages[2] = load_page(2)
-        pages[3] = load_page(3)
+        raw_all = sbuf("w1s23raw", [2, PACK, 2 * P], F32, "R5")
+        raw23 = [load_w1_columns("", a, 2 * P, 2 * P, raw_all[:, a]) for a in range(2)]
+        raw23.append(load_w1_columns("w1s23last", 2, 2 * P, 2 * P, "X0"))
+        pages[1] = load_plain_page(1)
+        w2_planes.append(load_scales("w2_plane1", w2_scales[:, :, BLOCK:], KP, BLOCK, nc.sync))
+        w2late = load_w2_columns("w2late", BLOCK, BLOCK)
+        for a in range(KP):
+            w1raw[a, 1] = load_rows("w1raw%d1" % a, w1, a, 1, "R%d" % a)
+        pages[2] = load_plain_page(2)
+        g1 = sbuf("g1", [PACK], F32)
+        nc.sync.dma_start(out=g1[:], in_=gain1[BLOCK:].rearrange("(p t) -> p t", t=PACK))
 
-        turned = bank("wgs_turned", "ab0")
+        wg1 = []
+        for s in range(PACK):
+            tile = sbuf("wg1_%d" % s, [S], F32, "G%d" % s)
+            nc.scalar.activation(tile[:], wgs_rows[:], ACT.Copy, scale=g1rows[:, s : s + 1])
+            wg1.append(tile)
+
+        turned = bank("wgs_turned", "ab3")
         for c in range(CH):
             nc.tensor.transpose(turned[:, c * P : (c + 1) * P], wgs_rows[:, c * P : (c + 1) * P], ident[:])
         spread = []
@@ -172,7 +201,7 @@ def tile_list_truffle_survey_walk_kernel(
             spread.append(tile)
         wg = sbuf("wg", [PACK, S], F32)
         for t in range(PACK):
-            acc = bank("wg_bank%d" % t, "hh%d" % t)
+            acc = bank("wg_bank%d" % t, ("hh3", "hh2", "ab2", "hh1")[t])
             for c in range(CH):
                 nc.tensor.transpose(acc[:, c * P : (c + 1) * P], spread[c][:, t].rearrange("p r q -> p (r q)"), ident[:])
             nc.scalar.copy(wg[:, t, :], acc[:])
@@ -182,16 +211,17 @@ def tile_list_truffle_survey_walk_kernel(
 
         def abs_product(b, banks):
             mags = []
+            mag_all = sbuf("mags", [CH, PACK, P], F32, "R1")
             for c in range(CH):
                 acc = bank("bT%d%d" % (b, c), banks % c)
                 cols = slice(c * P, (c + 1) * P)
                 for a in range(KP):
                     nc.tensor.matmul_mx(
                         out=acc[:], lhsT=vw[a][:, cols].bitcast(FP8X4), lhsT_scale=vs[a][:, cols],
-                        rhs=w2w[b][:, a, :].bitcast(FP4X4), rhs_scale=w2_plane[:, a, b * BLOCK : (b + 1) * BLOCK],
+                        rhs=w2late[:, a, :].bitcast(FP4X4), rhs_scale=w2_planes[b][:, a, :],
                         start=(a == 0), stop=(a == KP - 1),
                     )
-                mag = sbuf("mag%d%d" % (b, c), [PACK, P], F32, "B%d" % c)
+                mag = mag_all[:, c]
                 nc.scalar.activation(mag[:], dealt_view(acc), ACT.Abs)
                 mags.append(mag)
             return mags
@@ -232,51 +262,95 @@ def tile_list_truffle_survey_walk_kernel(
         def state(b, t, sums, h=None):
             if h is None:
                 h = sbuf("h%d%d" % (b, t), [S], F32, "h%d" % ((PACK * b + t) % 6))
-            nc.scalar.activation(h[:], sums[t][:], ACT.Copy, scale=g1[:, b, t : t + 1])
+            nc.scalar.activation(h[:], sums[t][:], ACT.Copy, scale=g1[:, t : t + 1])
             return h
 
         def put(s, h):
-            nc.vector.tensor_tensor(pages[s][:].indirect(idx2[:]), h[:], wg[:, s % PACK, :], MULT)
+            nc.vector.tensor_tensor(pages[s][:].indirect(idx2[:]), h[:], wg1[s][:] if s < PACK else wg[:, s - PACK, :], MULT)
 
         def recall(s, half, x):
             nc.vector.tensor_copy(x[:, s % PACK, :], pages[s][:].indirect(idx3[:, half * LCOL : (half + 1) * LCOL]))
 
-        accs = [bank("aT0%d" % c, "ab%d" % c) for c in range(CH)]
-        for a in range(KP - 1):
-            woven = weave(nc.vector.tensor_copy, "w1wv%d0" % a, w1raw[a, 0], "H%d" % a)
-            w1_pass(accs, a, quantize("w1q%d0" % a, woven))
-        for u in range(2):
-            woven = weave((nc.scalar.copy, nc.vector.tensor_copy)[u], "w1lastwv%d" % u, last_raw[u], "h%d" % (4 + u))
-            w1_pass(accs, KP - 1, quantize("w1lastq%d" % u, woven), u * HALF)
-        sums = open_sums(0, abs_product(0, "hh%d"))
-        hs = linear_part(0, accs, sums, (nc.scalar.copy, nc.vector.tensor_copy))
-        hs.append(state(0, 1, sums))
+        def plain_abs(s):
+            acc = bank("b%d" % s, "hh%d" % s)
+            words, first = (w2first, 0) if s == 0 else (w2rest, (s - 1) * P)
+            for a in range(KP):
+                nc.tensor.matmul_mx(
+                    out=acc[:], lhsT=words[:, a, 2 * first : 2 * (first + P)].bitcast(FP4X4),
+                    lhsT_scale=w2_planes[0][:, a, s * P : (s + 1) * P],
+                    rhs=vw[a][:].bitcast(FP8X4), rhs_scale=vs[a][:], start=(a == 0), stop=(a == KP - 1),
+                )
+            mag = sbuf("h0%d" % s, [S], F32, "h%d" % s)
+            nc.scalar.activation(mag[:], acc[:], ACT.Abs)
+            return mag
 
-        w3raw[0, 0] = load_rows("w3raw00", w3, 0, 0, "R3")
-        w3raw[1, 0] = load_rows("w3raw10", w3, 1, 0, "R4")
-        pages[4] = load_page(4)
-        pages[5] = load_page(5)
-        w3raw[0, 1] = load_rows("w3raw01", w3, 0, 1, "R5")
-        pages[6] = load_page(6)
+        def plain_linear(s, quantised, first):
+            acc = bank("a%d" % s, "ab%d" % s)
+            for a in range(KP):
+                codes, scales = quantised[a]
+                nc.tensor.matmul_mx(
+                    out=acc[:], lhsT=codes[:, first : first + P].bitcast(FP8X4), lhsT_scale=scales[:, first : first + P],
+                    rhs=vw[a][:].bitcast(FP8X4), rhs_scale=vs[a][:], start=(a == 0), stop=(a == KP - 1),
+                )
+            return acc
+
+        def plain_weights(name, raws, copies, slot, last_slot):
+            width = raws[0].shape[2] * PACK
+            woven = sbuf(name + "wv", [KP - 1, width], BF16, slot)
+            tiles = [woven[:, a] for a in range(KP - 1)] + [last_slot]
+            return [quantize("%sq%d" % (name, a), weave(copies[a], name + "last", raws[a], tiles[a])) for a in range(KP)]
+
+        def plain_put(s, acc, mag, h, slot):
+            nc.vector.tensor_tensor(h[:], acc[:], mag[:], ADD)
+            put(s, h)
+            xn = sbuf("xn%d" % s, [S], F32, slot)
+            nc.vector.tensor_copy(xn[:], pages[s][:].indirect(idx3[:]))
+            return xn
+
+        def deal_rows(dealt, s, xn):
+            for t in range(PACK):
+                nc.sync.dma_start(out=dealt[32 * s : 32 * (s + 1), t, :], in_=xn[t:P:PACK, :])
 
         x = {}
-        x[0, 0] = sbuf("x00", [PACK, HALF], F32, "H0")
+        q0 = plain_weights("w1s0", raw0, (nc.scalar.copy, nc.vector.tensor_copy, nc.vector.tensor_copy), "H0", "W0")
+        mag0 = plain_abs(0)
+        acc0 = plain_linear(0, q0, 0)
+        q1 = plain_weights("w1s1", raw1, [nc.scalar.copy] * KP, "H1", "W1")
+        xn = [plain_put(0, acc0, mag0, mag0, "W1")]
+        mag1, mag2, mag3 = [plain_abs(s) for s in range(1, PACK)]
+        acc1 = plain_linear(1, q1, 0)
+        q23 = plain_weights("w1s23", raw23, [nc.scalar.copy] * KP, "H0", "W2")
+        xn.append(plain_put(1, acc1, mag1, mag1, "W2"))
+        acc2 = plain_linear(2, q23, 0)
+        xn.append(plain_put(2, acc2, mag2, mag2, "W0"))
+        acc3 = plain_linear(3, q23, P)
+
+        w3raw[0, 0] = load_rows("w3raw00", w3, 0, 0, "R3")
+        pages[3] = load_plain_page(3)
+        pages[4] = load_page(4)
+        w3raw[1, 0] = load_rows("w3raw10", w3, 1, 0, "R4")
+        pages[5] = load_page(5)
+        w3raw[0, 1] = load_rows("w3raw01", w3, 0, 1, "R5")
+
         pair = sbuf("w1wv_pair", [2, BLOCK * PACK], BF16, "AA")
         wovens = [weave(nc.scalar.copy, "", w1raw[a, 1], pair[:, a]) for a in range(2)]
-        hs.append(state(0, 2, sums, sbuf("h02", [S], F32, "R1")))
-        mags = abs_product(1, "ab%d")
+        mags = abs_product(1, "hh%d")
         wovens.append(weave(nc.scalar.copy, "w1wv21", w1raw[2, 1], "AB"))
-        late = sbuf("h0late", [S], F32, "R2")
-        hs.append(state(0, 3, sums, late))
-        sums = open_sums(1, mags)
         accs = [bank("aT1%d" % c, "ab%d" % c) for c in range(CH)]
-        for t in range(PACK):
-            for a in ((), (), (0, 1), (2,))[t]:
-                w1_pass(accs, a, quantize("w1q%d1" % a, wovens[a]))
-            put(t, hs[t])
-            recall(t, 0, x[0, 0])
+        qs = [quantize("w1q%d1" % a, wovens[a]) for a in range(KP)]
+        xn.append(plain_put(3, acc3, mag3, mag3, "W3"))
+        sums = open_sums(1, mags)
+        for a in range(KP):
+            w1_pass(accs, a, qs[a])
 
+        dealt = sbuf("x0", [PACK, S], F32, "R2")
+        x[0, 0], x[0, 1] = dealt[:, :, :HALF], dealt[:, :, HALF:]
+        pages[6] = load_page(6)
+        deal_rows(dealt, 0, xn[0])
+        deal_rows(dealt, 1, xn[1])
         w3raw[1, 1] = load_rows("w3raw11", w3, 1, 1, "R0")
+        deal_rows(dealt, 2, xn[2])
+        deal_rows(dealt, 3, xn[3])
         pages[7] = load_page(7)
         g2 = sbuf("g2", [HB, PACK], F32)
         nc.sync.dma_start(out=g2[:], in_=gain2.rearrange("(b p t) -> p b t", b=HB, t=PACK))
@@ -287,10 +361,14 @@ def tile_list_truffle_survey_walk_kernel(
         wo = sbuf("wo", [S], F32)
         nc.sync.dma_start(out=wo[:], in_=wgo)
         walk = []
-        for n in range(NT):
-            tile = sbuf("walk%d" % n, [T2], F32)
+
+        def load_walk(n, slot):
+            tile = sbuf("walk%d" % n, [T2], F32, slot)
             nc.sync.dma_start(out=tile[:], in_=page1[n * P : (n + 1) * P, :])
             walk.append(tile)
+
+        for n in range(NT):
+            load_walk(n, (None, None, None, "R3", "R4")[n])
 
         hs = linear_part(1, accs, sums, (nc.scalar.copy, nc.scalar.copy))
         hs.extend(state(1, t, sums) for t in range(1, PACK))
@@ -306,29 +384,37 @@ def tile_list_truffle_survey_walk_kernel(
             put(PACK + t, hs[t])
             recall(PACK + t, 0, x[1, 0])
             if t == 1:
-                xq[0, 0] = quantize("xq00", weave(nc.scalar.copy, "xwv00", x[0, 0], "h5"))
-            if t == 2:
+                w3wv[0, 1] = weave_dealt("w3wv01", w3raw[0, 1], "H0")
                 w3wv[1, 1] = weave_dealt("w3wv11", w3raw[1, 1], "AB")
-                w3wv[0, 1] = weave_dealt("w3wv01", w3raw[0, 1], "h0")
+                xwv00 = weave(nc.scalar.copy, "xwv00", x[0, 0], "h5")
         xwv10 = weave(nc.scalar.copy, "xwv10", x[1, 0], "X0")
-        w3q = {key: quantize("w3q%d%d" % key, w3wv[key]) for key in w3wv}
+        planes = sbuf("late_planes", [5, BLOCK], U8, "h1")
+        w3q = {(0, 0): quantize("w3q00", w3wv[0, 0], planes[:, 0])}
+        xq[0, 0] = quantize("xq00", xwv00, planes[:, 4, :HALF])
+        w3q[1, 0] = quantize("w3q10", w3wv[1, 0], planes[:, 1])
         xq[1, 0] = quantize("xq10", xwv10)
+        for a in range(HB):
+            w3q[a, 1] = quantize("w3q%d1" % a, w3wv[a, 1], planes[:, 2 + a])
 
-        def stage2(half, k):
-            b, pair = divmod(k, 2)
-            acc = bank("e%d%d" % (half, k), "ab%d" % k)
-            for u in range(2):
-                cols = slice((2 * pair + u) * P, (2 * pair + u + 1) * P)
-                for a in range(HB):
-                    nc.tensor.matmul_mx(
-                        out=acc[:, u * HALF : (u + 1) * HALF],
-                        lhsT=w3q[a, b][0][:, cols].bitcast(FP8X4), lhsT_scale=w3q[a, b][1][:, cols],
-                        rhs=xq[a, half][0][:].bitcast(FP8X4), rhs_scale=xq[a, half][1][:],
-                        start=(a == 0), stop=(a == HB - 1),
-                    )
-            th = sbuf("tanh%d%d" % (half, k), [2, HALF], F32, "B%d" % k)
-            nc.scalar.activation(th[:].rearrange("p u j -> p (u j)"), acc[:], ACT.Tanh)
-            return th
+        def stage2(half):
+            accs = [bank("e%d%d" % (half, k), "ab%d" % k) for k in range(4)]
+            ths = []
+            for a in range(HB):
+                for k in range(4):
+                    b, pair = divmod(k, 2)
+                    for u in range(2):
+                        cols = slice((2 * pair + u) * P, (2 * pair + u + 1) * P)
+                        nc.tensor.matmul_mx(
+                            out=accs[k][:, u * HALF : (u + 1) * HALF],
+                            lhsT=w3q[a, b][0][:, cols].bitcast(FP8X4), lhsT_scale=w3q[a, b][1][:, cols],
+                            rhs=xq[a, half][0][:].bitcast(FP8X4), rhs_scale=xq[a, half][1][:],
+                            start=(a == 0 and u == 0), stop=(a == HB - 1 and u == 1),
+                        )
+            for k in range(4):
+                th = sbuf("tanh%d%d" % (half, k), [2, HALF], F32, "B%d" % k)
+                nc.scalar.activation(th[:].rearrange("p u j -> p (u j)"), accs[k][:], ACT.Tanh)
+                ths.append(th)
+            return ths
 
         def combine(half, k, th, z):
             b, pair = divmod(k, 2)
@@ -359,10 +445,7 @@ def tile_list_truffle_survey_walk_kernel(
                 walk[n][:].indirect(idx4[:, half * LCOL : (half + 1) * LCOL]), y[:], wo[:, half * HALF : (half + 1) * HALF], MULT
             )
 
-        ths = [stage2(0, k) for k in range(4)]
-        x[0, 1] = sbuf("x01", [PACK, HALF], F32, "X0")
-        for t in range(PACK):
-            recall(t, 1, x[0, 1])
+        ths = stage2(0)
         z0 = sbuf("z00", [PACK, HALF], BF16, "h2")
         z1 = sbuf("z10", [PACK, HALF], BF16, "h3")
         combine(0, 0, ths[0], z0)
@@ -370,20 +453,23 @@ def tile_list_truffle_survey_walk_kernel(
         zwv0 = weave(nc.scalar.copy, "zwv00", z0, "h4")
         combine(0, 2, ths[2], z1)
         combine(0, 3, ths[3], z1)
-        zwv1 = weave(nc.scalar.copy, "zwv10", z1, "h5")
+        flat = sbuf("x11", [PACK * HALF], F32, "H1")
+        x[1, 1] = flat[:].rearrange("p (t j) -> p t j", t=PACK)
+        zwv1 = weave(nc.scalar.copy, "", z1, flat[:, 2 * HALF :].bitcast(BF16))
         zq[0, 0] = quantize("zq00", zwv0)
-        x[1, 1] = sbuf("x11", [PACK, HALF], F32, "H1")
-        for t in range(PACK):
+        for t in range(2):
             recall(PACK + t, 1, x[1, 1])
         zq[1, 0] = quantize("zq10", zwv1)
+        for t in range(2, PACK):
+            recall(PACK + t, 1, x[1, 1])
         xq[0, 1] = quantize("xq01", weave(nc.scalar.copy, "xwv01", x[0, 1], "h3"))
         yacc = [stage3(0, n, "hh%d" % n) for n in range(4)]
-        place(0, 0, leave(0, 0, yacc[0], "Y0"))
+        place(0, 0, leave(0, 0, yacc[0], "G0"))
         yacc.append(stage3(0, 4, "hh0"))
-        place(0, 1, leave(0, 1, yacc[1], "Y1"))
+        place(0, 1, leave(0, 1, yacc[1], "G1"))
         xq[1, 1] = quantize("xq11", weave(nc.scalar.copy, "xwv11", x[1, 1], "h0"))
-        place(0, 2, leave(0, 2, yacc[2], "Y2"))
-        ths = [stage2(1, k) for k in range(4)]
+        place(0, 2, leave(0, 2, yacc[2], "G2"))
+        ths = stage2(1)
         z0 = sbuf("z01", [PACK, HALF], BF16, "h1")
         z1 = sbuf("z11", [PACK, HALF], BF16, "h2")
         combine(1, 0, ths[0], z0)
@@ -399,5 +485,5 @@ def tile_list_truffle_survey_walk_kernel(
         place(0, 4, leave(0, 4, yacc[4], "h2"))
         for n in range(NT):
             acc = stage3(1, n, "hh%d" % ((n + 1) % 4))
-            place(1, n, leave(1, n, acc, ("Y0", "Y1", "Y2", "B0", "B1")[n]))
+            place(1, n, leave(1, n, acc, ("G0", "G1", "G2", "B0", "B1")[n]))
             nc.sync.dma_start(out=out[n * P : (n + 1) * P, :], in_=walk[n][:])

@@ -137,9 +137,9 @@ def tile_list_truffle_survey_walk_kernel(
         idx = load_list("idx", offs)
         wgs_rows = sbuf("wgs_rows", [S], F32)
         nc.sync.dma_start(out=wgs_rows[:], in_=wgs)
-        g1rows = sbuf("g1rows", [PACK], F32)
-        with nc.allow_non_contiguous_dma(reason="one gain for each partition and slice"):
-            nc.sync.dma_start(out=g1rows[:], in_=gain1[:BLOCK].rearrange("(s p) -> p s", p=P))
+        gain_rows = sbuf("gain_rows", [P], F32)
+        nc.gpsimd.memset(gain_rows[:], 0.0)
+        nc.sync.dma_start(out=gain_rows[0:PACK, :], in_=gain1[:BLOCK].rearrange("(s p) -> s p", p=P))
         tab_plane = load_scales("tab_plane", tab_scales, KP, T, nc.sync)
         load_tab(0)
         load_tab(1)
@@ -169,18 +169,23 @@ def tile_list_truffle_survey_walk_kernel(
         raw_all = sbuf("w1s1raw", [KP, PACK, P], F32, "R4")
         raw1 = [load_w1_columns("", a, P, P, raw_all[:, a]) for a in range(KP)]
         idx3 = load_list("idx3", offs3)
+        pages[1] = load_plain_page(1)
         raw_all = sbuf("w1s23raw", [2, PACK, 2 * P], F32, "R5")
         raw23 = [load_w1_columns("", a, 2 * P, 2 * P, raw_all[:, a]) for a in range(2)]
         raw23.append(load_w1_columns("w1s23last", 2, 2 * P, 2 * P, "X0"))
-        pages[1] = load_plain_page(1)
         w2_planes.append(load_scales("w2_plane1", w2_scales[:, :, BLOCK:], KP, BLOCK, nc.sync))
         w2late = load_w2_columns("w2late", BLOCK, BLOCK)
-        for a in range(KP):
-            w1raw[a, 1] = load_rows("w1raw%d1" % a, w1, a, 1, "R%d" % a)
         pages[2] = load_plain_page(2)
+        w1raw[0, 1] = load_rows("w1raw01", w1, 0, 1, "R0")
+        w1raw[1, 1] = load_rows("w1raw11", w1, 1, 1, "R1")
+        w1raw[2, 1] = load_rows("w1raw21", w1, 2, 1, "R2")
         g1 = sbuf("g1", [PACK], F32)
         nc.sync.dma_start(out=g1[:], in_=gain1[BLOCK:].rearrange("(p t) -> p t", t=PACK))
 
+        gain_bank = bank("gain_turned", "ab2")
+        nc.tensor.transpose(gain_bank[:, :P], gain_rows[:], ident[:])
+        g1rows = sbuf("g1cols", [PACK], F32)
+        nc.scalar.copy(g1rows[:], gain_bank[:, :PACK])
         wg1 = []
         for s in range(PACK):
             tile = sbuf("wg1_%d" % s, [S], F32, "G%d" % s)
@@ -228,9 +233,8 @@ def tile_list_truffle_survey_walk_kernel(
 
         def open_sums(b, mags):
             sums = [bank("hsum%d%d" % (b, t), "hh%d" % t) for t in range(PACK)]
-            for t in range(PACK):
-                for c in range(CH):
-                    add_turned(sums[t], mags[c], t, c, c == 0, False)
+            for c in range(CH):
+                add_turned(sums[0], mags[c], 0, c, c == 0, False)
             return sums
 
         def w1_pass(accs, a, quantised, first=0):
@@ -256,7 +260,8 @@ def tile_list_truffle_survey_walk_kernel(
                 nc.scalar.copy(lin[:, c, 1:], dealt_view(accs[c])[:, 1:])
             for t in range(1, PACK):
                 for c in range(CH):
-                    add_turned(sums[t], lin[:, c], t, c, False, c == CH - 1)
+                    add_turned(sums[t], lin[:, c], t, c, c == 0, False)
+                    add_turned(sums[t], mags[c], t, c, False, c == CH - 1)
             return hs
 
         def state(b, t, sums, h=None):
@@ -325,8 +330,8 @@ def tile_list_truffle_survey_walk_kernel(
         xn.append(plain_put(2, acc2, mag2, mag2, "W0"))
         acc3 = plain_linear(3, q23, P)
 
-        w3raw[0, 0] = load_rows("w3raw00", w3, 0, 0, "R3")
         pages[3] = load_plain_page(3)
+        w3raw[0, 0] = load_rows("w3raw00", w3, 0, 0, "R3")
         pages[4] = load_page(4)
         w3raw[1, 0] = load_rows("w3raw10", w3, 1, 0, "R4")
         pages[5] = load_page(5)
@@ -334,8 +339,11 @@ def tile_list_truffle_survey_walk_kernel(
 
         pair = sbuf("w1wv_pair", [2, BLOCK * PACK], BF16, "AA")
         wovens = [weave(nc.scalar.copy, "", w1raw[a, 1], pair[:, a]) for a in range(2)]
+        last = sbuf("w1wv21", [2, HALF * PACK], BF16, "AB")
+        for u, copy in enumerate((nc.scalar.copy, nc.vector.tensor_copy)):
+            weave(copy, "", w1raw[2, 1][:, :, u * HALF : (u + 1) * HALF], last[:, u])
+        wovens.append(last[:].rearrange("p u c -> p (u c)"))
         mags = abs_product(1, "hh%d")
-        wovens.append(weave(nc.scalar.copy, "w1wv21", w1raw[2, 1], "AB"))
         accs = [bank("aT1%d" % c, "ab%d" % c) for c in range(CH)]
         qs = [quantize("w1q%d1" % a, wovens[a]) for a in range(KP)]
         xn.append(plain_put(3, acc3, mag3, mag3, "W3"))
@@ -346,12 +354,11 @@ def tile_list_truffle_survey_walk_kernel(
         dealt = sbuf("x0", [PACK, S], F32, "R2")
         x[0, 0], x[0, 1] = dealt[:, :, :HALF], dealt[:, :, HALF:]
         pages[6] = load_page(6)
-        deal_rows(dealt, 0, xn[0])
-        deal_rows(dealt, 1, xn[1])
         w3raw[1, 1] = load_rows("w3raw11", w3, 1, 1, "R0")
-        deal_rows(dealt, 2, xn[2])
-        deal_rows(dealt, 3, xn[3])
         pages[7] = load_page(7)
+        for t in range(PACK):
+            for s in (0, 2, 1, 3):
+                nc.sync.dma_start(out=dealt[32 * s : 32 * (s + 1), t, :], in_=xn[s][t:P:PACK, :])
         g2 = sbuf("g2", [HB, PACK], F32)
         nc.sync.dma_start(out=g2[:], in_=gain2.rearrange("(b p t) -> p b t", b=HB, t=PACK))
         idx4 = load_list("idx4", offs4)
@@ -387,14 +394,15 @@ def tile_list_truffle_survey_walk_kernel(
                 w3wv[0, 1] = weave_dealt("w3wv01", w3raw[0, 1], "H0")
                 w3wv[1, 1] = weave_dealt("w3wv11", w3raw[1, 1], "AB")
                 xwv00 = weave(nc.scalar.copy, "xwv00", x[0, 0], "h5")
-        xwv10 = weave(nc.scalar.copy, "xwv10", x[1, 0], "X0")
-        planes = sbuf("late_planes", [5, BLOCK], U8, "h1")
+        xwv10 = weave(nc.scalar.copy, "xwv10", x[1, 0], "W3")
+        planes = sbuf("late_planes", [2, BLOCK], U8, "h1")
         w3q = {(0, 0): quantize("w3q00", w3wv[0, 0], planes[:, 0])}
-        xq[0, 0] = quantize("xq00", xwv00, planes[:, 4, :HALF])
-        w3q[1, 0] = quantize("w3q10", w3wv[1, 0], planes[:, 1])
+        xq[0, 0] = quantize("xq00", xwv00, planes[:, 1, :HALF])
+        planes = sbuf("last_planes", [3, BLOCK], U8, "h5")
+        w3q[1, 0] = quantize("w3q10", w3wv[1, 0], planes[:, 2])
         xq[1, 0] = quantize("xq10", xwv10)
         for a in range(HB):
-            w3q[a, 1] = quantize("w3q%d1" % a, w3wv[a, 1], planes[:, 2 + a])
+            w3q[a, 1] = quantize("w3q%d1" % a, w3wv[a, 1], planes[:, a])
 
         def stage2(half):
             accs = [bank("e%d%d" % (half, k), "ab%d" % k) for k in range(4)]

@@ -27,6 +27,7 @@ NT = N // P
 CH = S // P
 HALF = S // 2
 LCOL = HALF // 16
+QUAD = P // PACK
 
 
 def tile_list_truffle_survey_walk_kernel(
@@ -38,13 +39,16 @@ def tile_list_truffle_survey_walk_kernel(
         sb = ctx.enter_context(tc.tile_pool(name="sb", bufs=1))
         ps = ctx.enter_context(tc.psum_pool(name="ps", bufs=1))
 
-        def sbuf(name, shape, dtype, slot=None):
-            return sb.tile([P] + shape, dtype, name=name, tag=slot or name, align_bytes=64)
+        def sbuf(name, shape, dtype, buffer=None):
+            return sb.tile([P] + shape, dtype, name=name, tag=buffer or name, align_bytes=64)
 
-        def bank(name, slot):
-            return ps.tile([P, BLOCK], F32, name=name, tag=slot)
+        def bank(name, which):
+            return ps.tile([P, BLOCK], F32, name=name, tag=which)
 
-        def load_scales(name, src, passes, width, queue):
+        def load(dst, src):
+            nc.sync.dma_start(out=dst, in_=src)
+
+        def load_scales(name, src, passes, width):
             plane = sbuf(name, [passes, width], U8)
             flat = plane[:].rearrange("p a c -> p (a c)").bitcast(I32)
             cut = flat.shape[1] // 2
@@ -52,7 +56,7 @@ def tile_list_truffle_survey_walk_kernel(
             nc.vector.memset(flat[:, cut:], 0)
             rows = src.rearrange("a (Q r) c -> r Q a c", r=4)
             for r in range(4):
-                queue.dma_start(out=plane[r:P:32].bitcast(I32), in_=rows[r].bitcast(I32))
+                load(plane[r:P:32].bitcast(I32), rows[r].bitcast(I32))
             return plane
 
         def load_list(name, src):
@@ -60,30 +64,34 @@ def tile_list_truffle_survey_walk_kernel(
             nc.sync.dma_start(lst[:], src)
             return lst
 
-        def load_rows(name, src, a, b, slot):
-            raw = sbuf(name, [PACK, BLOCK], F32, slot)
-            nc.sync.dma_start(
-                out=raw[:],
-                in_=src[a * BLOCK : (a + 1) * BLOCK, b * BLOCK : (b + 1) * BLOCK].rearrange("(p t) c -> p t c", t=PACK),
+        def load_rows(dst, src, a, first):
+            cols = slice(first, first + dst.shape[2])
+            load(dst, src[a * BLOCK : (a + 1) * BLOCK, cols].rearrange("(p t) c -> p t c", t=PACK))
+            return dst
+
+        def load_w2(name, first, width):
+            words = sbuf(name, [KP, 2 * width], U8)
+            load(
+                words[:].bitcast(I32),
+                w2_words.rearrange("a p c -> p a c")[:, :, 2 * first : 2 * (first + width)].bitcast(I32),
             )
-            return raw
+            return words
 
         def load_page(s):
-            b, t = divmod(s, PACK)
             tile = sbuf("page%d" % s, [T2], F32)
-            nc.sync.dma_start(out=tile[:], in_=page0[b * BLOCK : (b + 1) * BLOCK, :].rearrange("(p t) c -> t p c", t=PACK)[t])
+            if s < PACK:
+                load(tile[:], page0[s * P : (s + 1) * P, :])
+            else:
+                load(tile[:], page0[BLOCK:, :].rearrange("(p t) c -> t p c", t=PACK)[s - PACK])
             return tile
 
-        def weave(copy, name, src, slot):
-            width = src.shape[2]
-            woven = sbuf(name, [width * PACK], BF16, slot) if isinstance(slot, str) else slot
-            copy(woven[:].rearrange("p (c i t) -> p c t i", i=4, t=PACK), src[:].rearrange("p t (c i) -> p c t i", i=4))
+        def weave(copy, woven, src):
+            copy(woven.rearrange("p (c i t) -> p c t i", i=4, t=PACK), src.rearrange("p t (c i) -> p c t i", i=4))
             return woven
 
-        def weave_dealt(name, src, slot):
-            woven = sbuf(name, [BLOCK * PACK], BF16, slot) if isinstance(slot, str) else slot
+        def weave_dealt(woven, src):
             nc.scalar.copy(
-                woven[:].rearrange("p (u q t) -> p q t u", u=PACK, t=PACK), src[:].rearrange("p t (q u) -> p q t u", u=PACK)
+                woven.rearrange("p (u q t) -> p q t u", u=PACK, t=PACK), src.rearrange("p t (q u) -> p q t u", u=PACK)
             )
             return woven
 
@@ -92,205 +100,108 @@ def tile_list_truffle_survey_walk_kernel(
             codes = sbuf(name + "_codes", [width], U32)
             if scales is None:
                 scales = sbuf(name + "_scales", [width], U8)
-            nc.vector.quantize_mx(out=codes[:].bitcast(FP8X4), scales=scales[:], in_=woven[:])
+            nc.vector.quantize_mx(out=codes[:].bitcast(FP8X4), scales=scales[:], in_=woven)
             return codes, scales
 
-        def dealt_view(acc):
+        def by_slice(acc):
             return acc[:].rearrange("p (q t) -> p t q", t=PACK)
 
-        tab = []
-        for a in range(KP):
-            words = sbuf("tab%d" % a, [T], I32, "R%d" % a)
-            tab.append(words)
+        tab = [sbuf("tab%d" % a, [T], I32, "R%d" % a) for a in range(KP)]
 
         def load_tab(a):
-            nc.sync.dma_start(out=tab[a][:], in_=tab_words[a].rearrange("p n t -> p (n t)").bitcast(I32))
-
-        def load_w2(b):
-            words = sbuf("w2w%d" % b, [KP, 2 * BLOCK], U8)
-            nc.sync.dma_start(
-                out=words[:].bitcast(I32),
-                in_=w2_words.rearrange("a p c -> p a c")[:, :, 2 * BLOCK * b : 2 * BLOCK * (b + 1)].bitcast(I32),
-            )
-            return words
-
-        def load_w1_columns(name, a, first, width, slot):
-            raw = sbuf(name, [PACK, width], F32, slot) if isinstance(slot, str) else slot
-            nc.sync.dma_start(
-                out=raw[:], in_=w1[a * BLOCK : (a + 1) * BLOCK, first : first + width].rearrange("(p t) c -> p t c", t=PACK)
-            )
-            return raw
-
-        def load_w2_columns(name, first, width):
-            words = sbuf(name, [KP, 2 * width], U8)
-            nc.sync.dma_start(
-                out=words[:].bitcast(I32),
-                in_=w2_words.rearrange("a p c -> p a c")[:, :, 2 * first : 2 * (first + width)].bitcast(I32),
-            )
-            return words
-
-        def load_plain_page(s):
-            tile = sbuf("page%d" % s, [T2], F32)
-            nc.sync.dma_start(out=tile[:], in_=page0[s * P : (s + 1) * P, :])
-            return tile
+            load(tab[a][:], tab_words[a].rearrange("p n t -> p (n t)").bitcast(I32))
 
         idx = load_list("idx", offs)
         wgs_rows = sbuf("wgs_rows", [S], F32)
-        nc.sync.dma_start(out=wgs_rows[:], in_=wgs)
+        load(wgs_rows[:], wgs)
         gain_rows = sbuf("gain_rows", [P], F32)
         nc.gpsimd.memset(gain_rows[:], 0.0)
-        nc.sync.dma_start(out=gain_rows[0:PACK, :], in_=gain1[:BLOCK].rearrange("(s p) -> s p", p=P))
-        tab_plane = load_scales("tab_plane", tab_scales, KP, T, nc.sync)
+        load(gain_rows[0:PACK, :], gain1[:BLOCK].rearrange("(s p) -> s p", p=P))
+        tab_plane = load_scales("tab_plane", tab_scales, KP, T)
         load_tab(0)
         load_tab(1)
-        w2_planes = [load_scales("w2_plane0", w2_scales[:, :, :BLOCK], KP, BLOCK, nc.sync)]
+        w2_plane_plain = load_scales("w2_plane_plain", w2_scales[:, :, :BLOCK], KP, BLOCK)
         load_tab(2)
-        w2first = load_w2_columns("w2first", 0, P)
-        raw_all = sbuf("w1s0raw", [KP, PACK, P], F32, "R3")
-        raw0 = [load_w1_columns("", a, 0, P, raw_all[:, a]) for a in range(KP)]
+        w2_first = load_w2("w2_first", 0, P)
+        w1_01 = sbuf("w1_01", [2, KP, PACK, P], F32, "R3")
+        w1_0 = [load_rows(w1_01[:, 0, a], w1, a, 0) for a in range(KP)]
         ident = sbuf("ident", [P], F32)
         make_identity(nc, ident[:])
 
         vw, vs = [], []
         for a in range(KP):
-            words = sbuf("vw%d" % a, [S], U32)
-            nc.vector.tensor_copy(words[:], tab[a][:].bitcast(U32).indirect(idx[:]))
-            scales = sbuf("vs%d" % a, [S], U8)
-            nc.vector.tensor_copy(scales[:], tab_plane[:, a, :].indirect(idx[:]))
-            vw.append(words)
-            vs.append(scales)
+            vw.append(sbuf("vw%d" % a, [S], U32))
+            nc.vector.tensor_copy(vw[a][:], tab[a][:].bitcast(U32).indirect(idx[:]))
+            vs.append(sbuf("vs%d" % a, [S], U8))
+            nc.vector.tensor_copy(vs[a][:], tab_plane[:, a, :].indirect(idx[:]))
 
         pages = {}
-        w3raw = {}
-        w1raw = {}
         idx2 = load_list("idx2", offs2)
-        pages[0] = load_plain_page(0)
-        w2rest = load_w2_columns("w2rest", P, BLOCK - P)
-        raw_all = sbuf("w1s1raw", [KP, PACK, P], F32, "R4")
-        raw1 = [load_w1_columns("", a, P, P, raw_all[:, a]) for a in range(KP)]
+        pages[0] = load_page(0)
+        w2_rest = load_w2("w2_rest", P, BLOCK - P)
+        w1_1 = [load_rows(w1_01[:, 1, a], w1, a, P) for a in range(KP)]
         idx3 = load_list("idx3", offs3)
-        pages[1] = load_plain_page(1)
-        raw_all = sbuf("w1s23raw", [2, PACK, 2 * P], F32, "R5")
-        raw23 = [load_w1_columns("", a, 2 * P, 2 * P, raw_all[:, a]) for a in range(2)]
-        raw23.append(load_w1_columns("w1s23last", 2, 2 * P, 2 * P, "X0"))
-        w2_planes.append(load_scales("w2_plane1", w2_scales[:, :, BLOCK:], KP, BLOCK, nc.sync))
-        w2late = load_w2_columns("w2late", BLOCK, BLOCK)
-        pages[2] = load_plain_page(2)
-        w1raw[0, 1] = load_rows("w1raw01", w1, 0, 1, "R0")
-        w1raw[1, 1] = load_rows("w1raw11", w1, 1, 1, "R1")
-        w1raw[2, 1] = load_rows("w1raw21", w1, 2, 1, "R2")
-        g1 = sbuf("g1", [PACK], F32)
-        nc.sync.dma_start(out=g1[:], in_=gain1[BLOCK:].rearrange("(p t) -> p t", t=PACK))
+        pages[1] = load_page(1)
+        w1_23_all = sbuf("w1_23", [KP, PACK, 2 * P], F32, "R4")
+        w1_23 = [load_rows(w1_23_all[:, a], w1, a, 2 * P) for a in range(KP)]
+        pages[2] = load_page(2)
+        w2_plane_dealt = load_scales("w2_plane_dealt", w2_scales[:, :, BLOCK:], KP, BLOCK)
+        w2_dealt = load_w2("w2_dealt", BLOCK, BLOCK)
+        w1_dealt = [load_rows(sbuf("w1_dealt%d" % a, [PACK, BLOCK], F32, "R%d" % a)[:], w1, a, BLOCK) for a in range(KP)]
+        g1_dealt = sbuf("g1_dealt", [PACK], F32)
+        load(g1_dealt[:], gain1[BLOCK:].rearrange("(p t) -> p t", t=PACK))
 
         gain_bank = bank("gain_turned", "ab2")
         nc.tensor.transpose(gain_bank[:, :P], gain_rows[:], ident[:])
-        g1rows = sbuf("g1cols", [PACK], F32)
-        nc.scalar.copy(g1rows[:], gain_bank[:, :PACK])
-        wg1 = []
+        g1_plain = sbuf("g1_plain", [PACK], F32)
+        nc.scalar.copy(g1_plain[:], gain_bank[:, :PACK])
+        factors = []
         for s in range(PACK):
-            tile = sbuf("wg1_%d" % s, [S], F32, "G%d" % s)
-            nc.scalar.activation(tile[:], wgs_rows[:], ACT.Copy, scale=g1rows[:, s : s + 1])
-            wg1.append(tile)
+            factors.append(sbuf("factor%d" % s, [S], F32, "G%d" % s)[:])
+            nc.scalar.activation(factors[s], wgs_rows[:], ACT.Copy, scale=g1_plain[:, s : s + 1])
 
         turned = bank("wgs_turned", "ab3")
         for c in range(CH):
             nc.tensor.transpose(turned[:, c * P : (c + 1) * P], wgs_rows[:, c * P : (c + 1) * P], ident[:])
-        spread = []
-        spread_all = sbuf("spread", [CH, PACK, 4, 32], F32, "AA")
+        spread = sbuf("spread", [CH, PACK, PACK, QUAD], F32, "AA")
         for c in range(CH):
-            tile = spread_all[:, c]
-            nc.scalar.copy(
-                tile[:],
-                turned[:, c * P : (c + 1) * P].rearrange("p (q t) -> p t q", t=PACK).unsqueeze(2).to_broadcast([P, PACK, 4, 32]),
-            )
-            spread.append(tile)
-        wg = sbuf("wg", [PACK, S], F32)
-        for t in range(PACK):
-            acc = bank("wg_bank%d" % t, ("hh3", "hh2", "ab2", "hh1")[t])
+            rows = turned[:, c * P : (c + 1) * P].rearrange("p (q t) -> p t q", t=PACK)
+            nc.scalar.copy(spread[:, c], rows.unsqueeze(2).to_broadcast([P, PACK, PACK, QUAD]))
+        wgs_dealt = sbuf("wgs_dealt", [PACK, S], F32)
+        for t, which in enumerate(("hh3", "hh2", "ab2", "hh1")):
+            acc = bank("wgs_back%d" % t, which)
             for c in range(CH):
-                nc.tensor.transpose(acc[:, c * P : (c + 1) * P], spread[c][:, t].rearrange("p r q -> p (r q)"), ident[:])
-            nc.scalar.copy(wg[:, t, :], acc[:])
-
-        def add_turned(acc, src, t, c, start, stop):
-            nc.tensor.matmul(acc[:, c * P : (c + 1) * P], src[:, t, :], ident[:], start=start, stop=stop, is_transpose=True)
-
-        def abs_product(b, banks):
-            mags = []
-            mag_all = sbuf("mags", [CH, PACK, P], F32, "R1")
-            for c in range(CH):
-                acc = bank("bT%d%d" % (b, c), banks % c)
-                cols = slice(c * P, (c + 1) * P)
-                for a in range(KP):
-                    nc.tensor.matmul_mx(
-                        out=acc[:], lhsT=vw[a][:, cols].bitcast(FP8X4), lhsT_scale=vs[a][:, cols],
-                        rhs=w2late[:, a, :].bitcast(FP4X4), rhs_scale=w2_planes[b][:, a, :],
-                        start=(a == 0), stop=(a == KP - 1),
-                    )
-                mag = mag_all[:, c]
-                nc.scalar.activation(mag[:], dealt_view(acc), ACT.Abs)
-                mags.append(mag)
-            return mags
-
-        def open_sums(b, mags):
-            sums = [bank("hsum%d%d" % (b, t), "hh%d" % t) for t in range(PACK)]
-            for c in range(CH):
-                add_turned(sums[0], mags[c], 0, c, c == 0, False)
-            return sums
-
-        def w1_pass(accs, a, quantised, first=0):
-            codes, scales = quantised
-            end = first + codes.shape[1]
-            for c in range(CH):
-                cols = slice(c * P, (c + 1) * P)
-                nc.tensor.matmul_mx(
-                    out=accs[c][:, first:end], lhsT=vw[a][:, cols].bitcast(FP8X4), lhsT_scale=vs[a][:, cols],
-                    rhs=codes[:].bitcast(FP8X4), rhs_scale=scales[:],
-                    start=(a == 0), stop=(a == KP - 1 and end == BLOCK),
-                )
-
-        def linear_part(b, accs, sums, copies):
-            first = sbuf("linfirst%d" % b, [CH, 1, P], F32, "AA")
-            for c in range(CH):
-                copies[c % 2](first[:, c, 0], dealt_view(accs[c])[:, 0])
-            for c in range(CH):
-                add_turned(sums[0], first[:, c], 0, c, False, c == CH - 1)
-            hs = [state(b, 0, sums)]
-            lin = sbuf("lin%d" % b, [CH, PACK, P], F32, "AA")
-            for c in range(CH):
-                nc.scalar.copy(lin[:, c, 1:], dealt_view(accs[c])[:, 1:])
-            for t in range(1, PACK):
-                for c in range(CH):
-                    add_turned(sums[t], lin[:, c], t, c, c == 0, False)
-                    add_turned(sums[t], mags[c], t, c, False, c == CH - 1)
-            return hs
-
-        def state(b, t, sums, h=None):
-            if h is None:
-                h = sbuf("h%d%d" % (b, t), [S], F32, "h%d" % ((PACK * b + t) % 6))
-            nc.scalar.activation(h[:], sums[t][:], ACT.Copy, scale=g1[:, t : t + 1])
-            return h
+                nc.tensor.transpose(acc[:, c * P : (c + 1) * P], spread[:, c, t].rearrange("p r q -> p (r q)"), ident[:])
+            nc.scalar.copy(wgs_dealt[:, t, :], acc[:])
+            factors.append(wgs_dealt[:, t, :])
 
         def put(s, h):
-            nc.vector.tensor_tensor(pages[s][:].indirect(idx2[:]), h[:], wg1[s][:] if s < PACK else wg[:, s - PACK, :], MULT)
+            nc.vector.tensor_tensor(pages[s][:].indirect(idx2[:]), h[:], factors[s], MULT)
 
-        def recall(s, half, x):
-            nc.vector.tensor_copy(x[:, s % PACK, :], pages[s][:].indirect(idx3[:, half * LCOL : (half + 1) * LCOL]))
+        def plain_weights(name, rows, copies, buffer, last_buffer):
+            width = rows[0].shape[2] * PACK
+            first = sbuf(name + "_woven", [KP - 1, width], BF16, buffer)
+            quantised = []
+            for a in range(KP):
+                woven = first[:, a] if a < KP - 1 else sbuf(name + "_last", [width], BF16, last_buffer)[:]
+                quantised.append(quantize("%s_q%d" % (name, a), weave(copies[a], woven, rows[a])))
+            return quantised
 
         def plain_abs(s):
             acc = bank("b%d" % s, "hh%d" % s)
-            words, first = (w2first, 0) if s == 0 else (w2rest, (s - 1) * P)
+            words, first = (w2_first, 0) if s == 0 else (w2_rest, (s - 1) * P)
             for a in range(KP):
                 nc.tensor.matmul_mx(
                     out=acc[:], lhsT=words[:, a, 2 * first : 2 * (first + P)].bitcast(FP4X4),
-                    lhsT_scale=w2_planes[0][:, a, s * P : (s + 1) * P],
+                    lhsT_scale=w2_plane_plain[:, a, s * P : (s + 1) * P],
                     rhs=vw[a][:].bitcast(FP8X4), rhs_scale=vs[a][:], start=(a == 0), stop=(a == KP - 1),
                 )
-            mag = sbuf("h0%d" % s, [S], F32, "h%d" % s)
+            mag = sbuf("mag%d" % s, [S], F32, "h%d" % s)
             nc.scalar.activation(mag[:], acc[:], ACT.Abs)
             return mag
 
-        def plain_linear(s, quantised, first):
-            acc = bank("a%d" % s, "ab%d" % s)
+        def plain_linear(s, which, quantised, first):
+            acc = bank("a%d" % s, which)
             for a in range(KP):
                 codes, scales = quantised[a]
                 nc.tensor.matmul_mx(
@@ -299,141 +210,164 @@ def tile_list_truffle_survey_walk_kernel(
                 )
             return acc
 
-        def plain_weights(name, raws, copies, slot, last_slot):
-            width = raws[0].shape[2] * PACK
-            woven = sbuf(name + "wv", [KP - 1, width], BF16, slot)
-            tiles = [woven[:, a] for a in range(KP - 1)] + [last_slot]
-            return [quantize("%sq%d" % (name, a), weave(copies[a], name + "last", raws[a], tiles[a])) for a in range(KP)]
+        def plain_put(s, acc, mag, buffer):
+            nc.vector.tensor_tensor(mag[:], acc[:], mag[:], ADD)
+            put(s, mag)
+            recalled = sbuf("x_plain%d" % s, [S], F32, buffer)
+            nc.vector.tensor_copy(recalled[:], pages[s][:].indirect(idx3[:]))
+            return recalled
 
-        def plain_put(s, acc, mag, h, slot):
-            nc.vector.tensor_tensor(h[:], acc[:], mag[:], ADD)
-            put(s, h)
-            xn = sbuf("xn%d" % s, [S], F32, slot)
-            nc.vector.tensor_copy(xn[:], pages[s][:].indirect(idx3[:]))
-            return xn
+        q0 = plain_weights("w1_0", w1_0, (nc.scalar.copy, nc.vector.tensor_copy, nc.vector.tensor_copy), "H0", "W0")
+        mags = [plain_abs(0)]
+        acc = plain_linear(0, "ab0", q0, 0)
+        q1 = plain_weights("w1_1", w1_1, [nc.scalar.copy] * KP, "H1", "W1")
+        x_plain = [plain_put(0, acc, mags[0], "W1")]
+        mags.extend(plain_abs(s) for s in range(1, PACK))
+        acc = plain_linear(1, "ab1", q1, 0)
+        q23 = plain_weights("w1_23", w1_23, [nc.scalar.copy] * KP, "H0", "W2")
+        x_plain.append(plain_put(1, acc, mags[1], "W2"))
+        acc = plain_linear(2, "ab2", q23, 0)
+        x_plain.append(plain_put(2, acc, mags[2], "W0"))
+        acc = plain_linear(3, "ab2", q23, P)
 
-        def deal_rows(dealt, s, xn):
-            for t in range(PACK):
-                nc.sync.dma_start(out=dealt[32 * s : 32 * (s + 1), t, :], in_=xn[t:P:PACK, :])
+        for s in range(PACK - 1, 2 * PACK):
+            pages[s] = load_page(s)
+        w3_rows = [load_rows(sbuf("w3_rows0", [PACK, H], F32, "R3")[:], w3, 0, 0)]
 
-        x = {}
-        q0 = plain_weights("w1s0", raw0, (nc.scalar.copy, nc.vector.tensor_copy, nc.vector.tensor_copy), "H0", "W0")
-        mag0 = plain_abs(0)
-        acc0 = plain_linear(0, q0, 0)
-        q1 = plain_weights("w1s1", raw1, [nc.scalar.copy] * KP, "H1", "W1")
-        xn = [plain_put(0, acc0, mag0, mag0, "W1")]
-        mag1, mag2, mag3 = [plain_abs(s) for s in range(1, PACK)]
-        acc1 = plain_linear(1, q1, 0)
-        q23 = plain_weights("w1s23", raw23, [nc.scalar.copy] * KP, "H0", "W2")
-        xn.append(plain_put(1, acc1, mag1, mag1, "W2"))
-        acc2 = plain_linear(2, q23, 0)
-        xn.append(plain_put(2, acc2, mag2, mag2, "W0"))
-        acc3 = plain_linear(3, q23, P)
+        def add_turned(acc, src, t, c, start, stop):
+            nc.tensor.matmul(acc[:, c * P : (c + 1) * P], src[:, c, t, :], ident[:], start=start, stop=stop, is_transpose=True)
 
-        pages[3] = load_plain_page(3)
-        w3raw[0, 0] = load_rows("w3raw00", w3, 0, 0, "R3")
-        pages[4] = load_page(4)
-        w3raw[1, 0] = load_rows("w3raw10", w3, 1, 0, "R4")
-        pages[5] = load_page(5)
-        w3raw[0, 1] = load_rows("w3raw01", w3, 0, 1, "R5")
-
-        pair = sbuf("w1wv_pair", [2, BLOCK * PACK], BF16, "AA")
-        wovens = [weave(nc.scalar.copy, "", w1raw[a, 1], pair[:, a]) for a in range(2)]
-        last = sbuf("w1wv21", [2, HALF * PACK], BF16, "AB")
+        pair = sbuf("w1_dealt_woven", [2, BLOCK * PACK], BF16, "AA")
+        woven = [weave(nc.scalar.copy, pair[:, a], w1_dealt[a]) for a in range(2)]
+        last = sbuf("w1_dealt_last", [2, HALF * PACK], BF16, "AB")
         for u, copy in enumerate((nc.scalar.copy, nc.vector.tensor_copy)):
-            weave(copy, "", w1raw[2, 1][:, :, u * HALF : (u + 1) * HALF], last[:, u])
-        wovens.append(last[:].rearrange("p u c -> p (u c)"))
-        mags = abs_product(1, "hh%d")
-        accs = [bank("aT1%d" % c, "ab%d" % c) for c in range(CH)]
-        qs = [quantize("w1q%d1" % a, wovens[a]) for a in range(KP)]
-        xn.append(plain_put(3, acc3, mag3, mag3, "W3"))
-        sums = open_sums(1, mags)
+            weave(copy, last[:, u], w1_dealt[2][:, :, u * HALF : (u + 1) * HALF])
+        woven.append(last[:].rearrange("p u c -> p (u c)"))
+        mag_turned = sbuf("mag_turned", [CH, PACK, P], F32, "R2")
+        for c in range(CH):
+            b_turned = bank("b_turned%d" % c, "hh%d" % c)
+            cols = slice(c * P, (c + 1) * P)
+            for a in range(KP):
+                nc.tensor.matmul_mx(
+                    out=b_turned[:], lhsT=vw[a][:, cols].bitcast(FP8X4), lhsT_scale=vs[a][:, cols],
+                    rhs=w2_dealt[:, a, :].bitcast(FP4X4), rhs_scale=w2_plane_dealt[:, a, :],
+                    start=(a == 0), stop=(a == KP - 1),
+                )
+            nc.scalar.activation(mag_turned[:, c], by_slice(b_turned), ACT.Abs)
+        a_turned = [bank("a_turned%d" % c, "ab%d" % ((c + 3) % CH)) for c in range(CH)]
+        q_dealt = [quantize("w1_dealt_q%d" % a, woven[a]) for a in range(KP)]
+        x_plain.append(plain_put(3, acc, mags[3], "W3"))
+        sums = [bank("sum%d" % t, "hh%d" % t) for t in range(PACK)]
+        for c in range(CH):
+            add_turned(sums[0], mag_turned, 0, c, c == 0, False)
         for a in range(KP):
-            w1_pass(accs, a, qs[a])
+            codes, scales = q_dealt[a]
+            for c in range(CH):
+                cols = slice(c * P, (c + 1) * P)
+                nc.tensor.matmul_mx(
+                    out=a_turned[c][:], lhsT=vw[a][:, cols].bitcast(FP8X4), lhsT_scale=vs[a][:, cols],
+                    rhs=codes[:].bitcast(FP8X4), rhs_scale=scales[:], start=(a == 0), stop=(a == KP - 1),
+                )
 
-        dealt = sbuf("x0", [PACK, S], F32, "R2")
-        x[0, 0], x[0, 1] = dealt[:, :, :HALF], dealt[:, :, HALF:]
-        pages[6] = load_page(6)
-        w3raw[1, 1] = load_rows("w3raw11", w3, 1, 1, "R0")
-        pages[7] = load_page(7)
+        x0 = sbuf("x0", [PACK, S], F32, "R1")
+        x = {(0, 0): x0[:, :, :HALF], (0, 1): x0[:, :, HALF:]}
+        w3_rows.append(load_rows(sbuf("w3_rows1", [PACK, H], F32, "R4")[:], w3, 1, 0))
         for t in range(PACK):
             for s in (0, 2, 1, 3):
-                nc.sync.dma_start(out=dealt[32 * s : 32 * (s + 1), t, :], in_=xn[s][t:P:PACK, :])
+                nc.sync.dma_start(out=x0[QUAD * s : QUAD * (s + 1), t, :], in_=x_plain[s][t:P:PACK, :])
+
         g2 = sbuf("g2", [HB, PACK], F32)
-        nc.sync.dma_start(out=g2[:], in_=gain2.rearrange("(b p t) -> p b t", b=HB, t=PACK))
+        load(g2[:], gain2.rearrange("(b p t) -> p b t", b=HB, t=PACK))
         idx4 = load_list("idx4", offs4)
-        w4_plane = load_scales("w4_plane", w4_scales, HB, N, nc.sync)
+        w4_plane = load_scales("w4_plane", w4_scales, HB, N)
         w4w = sbuf("w4w", [HB, N], I32)
-        nc.sync.dma_start(out=w4w[:], in_=w4_words.rearrange("a p n t -> p a (n t)").bitcast(I32))
+        load(w4w[:], w4_words.rearrange("a p n t -> p a (n t)").bitcast(I32))
         wo = sbuf("wo", [S], F32)
-        nc.sync.dma_start(out=wo[:], in_=wgo)
+        load(wo[:], wgo)
         walk = []
+        for n, buffer in enumerate((None, None, None, "R3", "R0")):
+            walk.append(sbuf("walk%d" % n, [T2], F32, buffer))
+            load(walk[n][:], page1[n * P : (n + 1) * P, :])
 
-        def load_walk(n, slot):
-            tile = sbuf("walk%d" % n, [T2], F32, slot)
-            nc.sync.dma_start(out=tile[:], in_=page1[n * P : (n + 1) * P, :])
-            walk.append(tile)
+        def state(t, buffer):
+            h = sbuf("h_dealt%d" % t, [S], F32, buffer)
+            nc.scalar.activation(h[:], sums[t][:], ACT.Copy, scale=g1_dealt[:, t : t + 1])
+            return h
 
-        for n in range(NT):
-            load_walk(n, (None, None, None, "R3", "R4")[n])
+        def recall(t, half):
+            window = pages[PACK + t][:].indirect(idx3[:, half * LCOL : (half + 1) * LCOL])
+            nc.vector.tensor_copy(x[1, half][:, t, :], window)
 
-        hs = linear_part(1, accs, sums, (nc.scalar.copy, nc.scalar.copy))
-        hs.extend(state(1, t, sums) for t in range(1, PACK))
-        x[1, 0] = sbuf("x10", [PACK, HALF], F32, "H1")
-        xq = {}
-        w3wv = {}
-        put(4, hs[0])
-        recall(4, 0, x[1, 0])
-        pair = sbuf("w3wv_pair", [2, BLOCK * PACK], BF16, "AA")
-        for a in range(HB):
-            w3wv[a, 0] = weave_dealt("", w3raw[a, 0], pair[:, a])
+        lin_first = sbuf("lin_first", [CH, 1, P], F32, "AA")
+        for c in range(CH):
+            nc.scalar.copy(lin_first[:, c, 0], by_slice(a_turned[c])[:, 0])
+        for c in range(CH):
+            add_turned(sums[0], lin_first, 0, c, False, c == CH - 1)
+        hs = [state(0, "h4")]
+        lin = sbuf("lin", [CH, PACK, P], F32, "AA")
+        for c in range(CH):
+            nc.scalar.copy(lin[:, c, 1:], by_slice(a_turned[c])[:, 1:])
         for t in range(1, PACK):
-            put(PACK + t, hs[t])
-            recall(PACK + t, 0, x[1, 0])
-            if t == 1:
-                w3wv[0, 1] = weave_dealt("w3wv01", w3raw[0, 1], "H0")
-                w3wv[1, 1] = weave_dealt("w3wv11", w3raw[1, 1], "AB")
-                xwv00 = weave(nc.scalar.copy, "xwv00", x[0, 0], "h5")
-        xwv10 = weave(nc.scalar.copy, "xwv10", x[1, 0], "W3")
-        planes = sbuf("late_planes", [2, BLOCK], U8, "h1")
-        w3q = {(0, 0): quantize("w3q00", w3wv[0, 0], planes[:, 0])}
-        xq[0, 0] = quantize("xq00", xwv00, planes[:, 1, :HALF])
-        planes = sbuf("last_planes", [3, BLOCK], U8, "h5")
-        w3q[1, 0] = quantize("w3q10", w3wv[1, 0], planes[:, 2])
-        xq[1, 0] = quantize("xq10", xwv10)
-        for a in range(HB):
-            w3q[a, 1] = quantize("w3q%d1" % a, w3wv[a, 1], planes[:, a])
+            for c in range(CH):
+                add_turned(sums[t], lin, t, c, c == 0, False)
+                add_turned(sums[t], mag_turned, t, c, False, c == CH - 1)
+        hs.extend(state(t, buffer) for t, buffer in ((1, "h5"), (2, "h0"), (3, "h1")))
 
-        def stage2(half):
+        x[1, 0] = sbuf("x10", [PACK, HALF], F32, "H1")[:]
+        put(PACK, hs[0])
+        recall(0, 0)
+        pair = sbuf("w3_woven", [HB, BLOCK * PACK], BF16, "AA")
+        w3_woven = {(a, 0): weave_dealt(pair[:, a], w3_rows[a][:, :, :BLOCK]) for a in range(HB)}
+        put(PACK + 1, hs[1])
+        for a, buffer in enumerate(("H0", "AB")):
+            w3_woven[a, 1] = weave_dealt(sbuf("w3_woven%d1" % a, [BLOCK * PACK], BF16, buffer)[:], w3_rows[a][:, :, BLOCK:])
+        x00_woven = weave(nc.scalar.copy, sbuf("x00_woven", [HALF * PACK], BF16, "h5")[:], x[0, 0])
+        for t in range(2, PACK):
+            put(PACK + t, hs[t])
+            recall(t - 1, 0)
+        recall(PACK - 1, 0)
+        x10_woven = weave(nc.scalar.copy, sbuf("x10_woven", [HALF * PACK], BF16, "W3")[:], x[1, 0])
+        planes = sbuf("planes_first", [2, BLOCK], U8, "h1")
+        w3q = {(0, 0): quantize("w3q00", w3_woven[0, 0], planes[:, 0])}
+        xq = {(0, 0): quantize("xq00", x00_woven, planes[:, 1, :HALF])}
+        planes = sbuf("planes_rest", [3, BLOCK], U8, "h5")
+        w3q[1, 0] = quantize("w3q10", w3_woven[1, 0], planes[:, 2])
+        xq[1, 0] = quantize("xq10", x10_woven)
+        for a in range(HB):
+            w3q[a, 1] = quantize("w3q%d1" % a, w3_woven[a, 1], planes[:, a])
+
+        def features(half):
             accs = [bank("e%d%d" % (half, k), "ab%d" % k) for k in range(4)]
-            ths = []
             for a in range(HB):
                 for k in range(4):
-                    b, pair = divmod(k, 2)
+                    b, first = k // 2, 2 * (k % 2)
                     for u in range(2):
-                        cols = slice((2 * pair + u) * P, (2 * pair + u + 1) * P)
+                        cols = slice((first + u) * P, (first + u + 1) * P)
                         nc.tensor.matmul_mx(
                             out=accs[k][:, u * HALF : (u + 1) * HALF],
                             lhsT=w3q[a, b][0][:, cols].bitcast(FP8X4), lhsT_scale=w3q[a, b][1][:, cols],
                             rhs=xq[a, half][0][:].bitcast(FP8X4), rhs_scale=xq[a, half][1][:],
                             start=(a == 0 and u == 0), stop=(a == HB - 1 and u == 1),
                         )
+            tanhs = []
             for k in range(4):
-                th = sbuf("tanh%d%d" % (half, k), [2, HALF], F32, "B%d" % k)
-                nc.scalar.activation(th[:].rearrange("p u j -> p (u j)"), accs[k][:], ACT.Tanh)
-                ths.append(th)
-            return ths
+                tanhs.append(sbuf("tanh%d%d" % (half, k), [2, HALF], F32, "B%d" % k))
+                nc.scalar.activation(tanhs[k][:].rearrange("p u j -> p (u j)"), accs[k][:], ACT.Tanh)
+            return tanhs
 
-        def combine(half, k, th, z):
-            b, pair = divmod(k, 2)
+        def combine(half, k, tanhs, z):
+            b, first = k // 2, 2 * (k % 2)
             for u in range(2):
-                t = 2 * pair + u
-                nc.vector.scalar_tensor_tensor(z[:, t, :], th[:, u, :], g2[:, b, t : t + 1], x[b, half][:, t, :], MULT, ADD)
+                t = first + u
+                nc.vector.scalar_tensor_tensor(z[:, t, :], tanhs[k][:, u, :], g2[:, b, t : t + 1], x[b, half][:, t, :], MULT, ADD)
+
+        def woven_tile(name, buffer):
+            return sbuf(name, [HALF * PACK], BF16, buffer)[:]
 
         zq = {}
 
-        def stage3(half, n, bank_slot):
-            acc = bank("y%d%d" % (half, n), bank_slot)
+        def last_product(half, n, which):
+            acc = bank("y%d%d" % (half, n), which)
             cols = slice(n * P, (n + 1) * P)
             for a in range(HB):
                 nc.tensor.matmul_mx(
@@ -443,55 +377,54 @@ def tile_list_truffle_survey_walk_kernel(
                 )
             return acc
 
-        def leave(half, n, acc, slot):
-            y = sbuf("ysb%d%d" % (half, n), [HALF], F32, slot)
+        def leave(half, n, acc, buffer):
+            y = sbuf("y_out%d%d" % (half, n), [HALF], F32, buffer)
             nc.scalar.copy(y[:], acc[:, :HALF])
             return y
 
         def place(half, n, y):
-            nc.vector.tensor_tensor(
-                walk[n][:].indirect(idx4[:, half * LCOL : (half + 1) * LCOL]), y[:], wo[:, half * HALF : (half + 1) * HALF], MULT
-            )
+            window = walk[n][:].indirect(idx4[:, half * LCOL : (half + 1) * LCOL])
+            nc.vector.tensor_tensor(window, y[:], wo[:, half * HALF : (half + 1) * HALF], MULT)
 
-        ths = stage2(0)
+        tanhs = features(0)
         z0 = sbuf("z00", [PACK, HALF], BF16, "h2")
         z1 = sbuf("z10", [PACK, HALF], BF16, "h3")
-        combine(0, 0, ths[0], z0)
-        combine(0, 1, ths[1], z0)
-        zwv0 = weave(nc.scalar.copy, "zwv00", z0, "h4")
-        combine(0, 2, ths[2], z1)
-        combine(0, 3, ths[3], z1)
-        flat = sbuf("x11", [PACK * HALF], F32, "H1")
-        x[1, 1] = flat[:].rearrange("p (t j) -> p t j", t=PACK)
-        zwv1 = weave(nc.scalar.copy, "", z1, flat[:, 2 * HALF :].bitcast(BF16))
-        zq[0, 0] = quantize("zq00", zwv0)
-        for t in range(2):
-            recall(PACK + t, 1, x[1, 1])
-        zq[1, 0] = quantize("zq10", zwv1)
-        for t in range(2, PACK):
-            recall(PACK + t, 1, x[1, 1])
-        xq[0, 1] = quantize("xq01", weave(nc.scalar.copy, "xwv01", x[0, 1], "h3"))
-        yacc = [stage3(0, n, "hh%d" % n) for n in range(4)]
-        place(0, 0, leave(0, 0, yacc[0], "G0"))
-        yacc.append(stage3(0, 4, "hh0"))
-        place(0, 1, leave(0, 1, yacc[1], "G1"))
-        xq[1, 1] = quantize("xq11", weave(nc.scalar.copy, "xwv11", x[1, 1], "h0"))
-        place(0, 2, leave(0, 2, yacc[2], "G2"))
-        ths = stage2(1)
+        combine(0, 0, tanhs, z0)
+        combine(0, 1, tanhs, z0)
+        z0_woven = weave(nc.scalar.copy, woven_tile("z00_woven", "h4"), z0[:])
+        combine(0, 2, tanhs, z1)
+        combine(0, 3, tanhs, z1)
+        x11 = sbuf("x11", [PACK * HALF], F32, "H1")
+        x[1, 1] = x11[:].rearrange("p (t j) -> p t j", t=PACK)
+        z1_woven = weave(nc.scalar.copy, x11[:, 2 * HALF :].bitcast(BF16), z1[:])
+        zq[0, 0] = quantize("zq00", z0_woven)
+        recall(0, 1)
+        recall(1, 1)
+        zq[1, 0] = quantize("zq10", z1_woven)
+        recall(2, 1)
+        recall(3, 1)
+        xq[0, 1] = quantize("xq01", weave(nc.scalar.copy, woven_tile("x01_woven", "h3"), x[0, 1]))
+        ys = [last_product(0, n, "hh%d" % n) for n in range(NT - 1)]
+        place(0, 0, leave(0, 0, ys[0], "G0"))
+        ys.append(last_product(0, NT - 1, "hh0"))
+        place(0, 1, leave(0, 1, ys[1], "G1"))
+        xq[1, 1] = quantize("xq11", weave(nc.scalar.copy, woven_tile("x11_woven", "h0"), x[1, 1]))
+        place(0, 2, leave(0, 2, ys[2], "G2"))
+
+        tanhs = features(1)
         z0 = sbuf("z01", [PACK, HALF], BF16, "h1")
         z1 = sbuf("z11", [PACK, HALF], BF16, "h2")
-        combine(1, 0, ths[0], z0)
-        combine(1, 1, ths[1], z0)
-        combine(1, 2, ths[2], z1)
-        y3 = leave(0, 3, yacc[3], "B2")
-        combine(1, 3, ths[3], z1)
-        zwv0 = weave(nc.scalar.copy, "zwv01", z0, "h4")
-        zwv1 = weave(nc.scalar.copy, "zwv11", z1, "h5")
+        combine(1, 0, tanhs, z0)
+        combine(1, 1, tanhs, z0)
+        combine(1, 2, tanhs, z1)
+        y3 = leave(0, 3, ys[3], "B2")
+        combine(1, 3, tanhs, z1)
+        z0_woven = weave(nc.scalar.copy, woven_tile("z01_woven", "h4"), z0[:])
+        z1_woven = weave(nc.scalar.copy, woven_tile("z11_woven", "h5"), z1[:])
         place(0, 3, y3)
-        zq[0, 1] = quantize("zq01", zwv0)
-        zq[1, 1] = quantize("zq11", zwv1)
-        place(0, 4, leave(0, 4, yacc[4], "h2"))
-        for n in range(NT):
-            acc = stage3(1, n, "hh%d" % ((n + 1) % 4))
-            place(1, n, leave(1, n, acc, ("G0", "G1", "G2", "B0", "B1")[n]))
+        zq[0, 1] = quantize("zq01", z0_woven)
+        zq[1, 1] = quantize("zq11", z1_woven)
+        place(0, 4, leave(0, 4, ys[4], "h2"))
+        for n, buffer in enumerate(("G0", "G1", "G2", "B0", "B1")):
+            place(1, n, leave(1, n, last_product(1, n, "hh%d" % ((n + 1) % 4)), buffer))
             nc.sync.dma_start(out=out[n * P : (n + 1) * P, :], in_=walk[n][:])

from contextlib import ExitStack

import concourse.mybir as mybir
from concourse.masks import make_identity

K, T, S, H, N, T2 = 1536, 2048, 512, 1024, 640, 1024
FLOPS = 2 * S * (2 * K * H + H * H + H * N)

F32 = mybir.dt.float32
BF16 = mybir.dt.bfloat16
I32 = mybir.dt.int32
U32 = mybir.dt.uint32
U16 = mybir.dt.uint16
U8 = mybir.dt.uint8
FP8X4 = mybir.dt.float8_e4m3fn_x4
FP4X4 = mybir.dt.float4_e2m1fn_x4
ACT = mybir.ActivationFunctionType
MULT = mybir.AluOpType.mult
ADD = mybir.AluOpType.add

P = 128
PACK = 4
BLOCK = P * PACK
KP = K // BLOCK
HB = H // BLOCK
NT = N // P
CH = S // P
HALF = S // 2
LCOL = HALF // 16
QUAD = P // PACK


def tile_list_truffle_survey_walk_kernel(
    tc, tab_words, tab_scales, offs, offs2, offs3, offs4, w1, w2_words, w2_scales, gain1,
    page0, wgs, w3, gain2, w4_words, w4_scales, page1, wgo, out,
):
    nc = tc.nc
    with ExitStack() as ctx:
        sb = ctx.enter_context(tc.tile_pool(name="sb", bufs=1))
        ps = ctx.enter_context(tc.psum_pool(name="ps", bufs=1))

        def sbuf(name, shape, dtype, buffer=None):
            return sb.tile([P] + shape, dtype, name=name, tag=buffer or name, align_bytes=64)

        def bank(name, which):
            return ps.tile([P, BLOCK], F32, name=name, tag=which)

        def load(dst, src):
            nc.sync.dma_start(out=dst, in_=src)

        def load_scales(name, src, passes, width):
            plane = sbuf(name, [passes, width], U8)
            flat = plane[:].rearrange("p a c -> p (a c)").bitcast(I32)
            cut = flat.shape[1] // 2
            nc.gpsimd.memset(flat[:, :cut], 0)
            nc.vector.memset(flat[:, cut:], 0)
            rows = src.rearrange("a (Q r) c -> r Q a c", r=4)
            for r in range(4):
                load(plane[r:P:32].bitcast(I32), rows[r].bitcast(I32))
            return plane

        def load_list(name, src):
            lst = sbuf(name, [S // 16], U16)
            nc.sync.dma_start(lst[:], src)
            return lst

        def load_rows(dst, src, a, first):
            cols = slice(first, first + dst.shape[2])
            load(dst, src[a * BLOCK : (a + 1) * BLOCK, cols].rearrange("(p t) c -> p t c", t=PACK))
            return dst

        def load_w2(name, first, width):
            words = sbuf(name, [KP, 2 * width], U8)
            load(
                words[:].bitcast(I32),
                w2_words.rearrange("a p c -> p a c")[:, :, 2 * first : 2 * (first + width)].bitcast(I32),
            )
            return words

        def load_page(s):
            tile = sbuf("page%d" % s, [T2], F32)
            if s < PACK:
                load(tile[:], page0[s * P : (s + 1) * P, :])
            else:
                load(tile[:], page0[BLOCK:, :].rearrange("(p t) c -> t p c", t=PACK)[s - PACK])
            return tile

        def weave(copy, woven, src):
            copy(woven.rearrange("p (c i t) -> p c t i", i=4, t=PACK), src.rearrange("p t (c i) -> p c t i", i=4))
            return woven

        def weave_dealt(woven, src):
            nc.scalar.copy(
                woven.rearrange("p (u q t) -> p q t u", u=PACK, t=PACK), src.rearrange("p t (q u) -> p q t u", u=PACK)
            )
            return woven

        def quantize(name, woven, scales=None):
            width = woven.shape[1] // PACK
            codes = sbuf(name + "_codes", [width], U32)
            if scales is None:
                scales = sbuf(name + "_scales", [width], U8)
            nc.vector.quantize_mx(out=codes[:].bitcast(FP8X4), scales=scales[:], in_=woven)
            return codes, scales

        def by_slice(acc):
            return acc[:].rearrange("p (q t) -> p t q", t=PACK)

        tab = [sbuf("tab%d" % a, [T], I32, "R%d" % a) for a in range(KP)]

        def load_tab(a):
            load(tab[a][:], tab_words[a].rearrange("p n t -> p (n t)").bitcast(I32))

        idx = load_list("idx", offs)
        wgs_rows = sbuf("wgs_rows", [S], F32)
        load(wgs_rows[:], wgs)
        gain_rows = sbuf("gain_rows", [P], F32)
        nc.gpsimd.memset(gain_rows[:], 0.0)
        load(gain_rows[0:PACK, :], gain1[:BLOCK].rearrange("(s p) -> s p", p=P))
        tab_plane = load_scales("tab_plane", tab_scales, KP, T)
        load_tab(0)
        load_tab(1)
        w2_plane_plain = load_scales("w2_plane_plain", w2_scales[:, :, :BLOCK], KP, BLOCK)
        load_tab(2)
        w2_first = load_w2("w2_first", 0, P)
        w1_01 = sbuf("w1_01", [2, KP, PACK, P], F32, "R3")
        w1_0 = [load_rows(w1_01[:, 0, a], w1, a, 0) for a in range(KP)]
        ident = sbuf("ident", [P], F32)
        make_identity(nc, ident[:])

        vw, vs = [], []
        for a in range(KP):
            vw.append(sbuf("vw%d" % a, [S], U32))
            nc.vector.tensor_copy(vw[a][:], tab[a][:].bitcast(U32).indirect(idx[:]))
            vs.append(sbuf("vs%d" % a, [S], U8))
            nc.vector.tensor_copy(vs[a][:], tab_plane[:, a, :].indirect(idx[:]))

        pages = {}
        idx2 = load_list("idx2", offs2)
        pages[0] = load_page(0)
        w2_rest = load_w2("w2_rest", P, BLOCK - P)
        w1_1 = [load_rows(w1_01[:, 1, a], w1, a, P) for a in range(KP)]
        idx3 = load_list("idx3", offs3)
        pages[1] = load_page(1)
        w1_23_all = sbuf("w1_23", [KP, PACK, 2 * P], F32, "R4")
        w1_23 = [load_rows(w1_23_all[:, a], w1, a, 2 * P) for a in range(KP)]
        pages[2] = load_page(2)
        w2_plane_dealt = load_scales("w2_plane_dealt", w2_scales[:, :, BLOCK:], KP, BLOCK)
        w2_dealt = load_w2("w2_dealt", BLOCK, BLOCK)
        w1_dealt = [load_rows(sbuf("w1_dealt%d" % a, [PACK, BLOCK], F32, "R%d" % a)[:], w1, a, BLOCK) for a in range(KP)]
        g1_dealt = sbuf("g1_dealt", [PACK], F32)
        load(g1_dealt[:], gain1[BLOCK:].rearrange("(p t) -> p t", t=PACK))

        gain_bank = bank("gain_turned", "ab2")
        nc.tensor.transpose(gain_bank[:, :P], gain_rows[:], ident[:])
        g1_plain = sbuf("g1_plain", [PACK], F32)
        nc.scalar.copy(g1_plain[:], gain_bank[:, :PACK])
        factors = []
        for s in range(PACK):
            factors.append(sbuf("factor%d" % s, [S], F32, "G%d" % s)[:])
            nc.scalar.activation(factors[s], wgs_rows[:], ACT.Copy, scale=g1_plain[:, s : s + 1])

        turned = bank("wgs_turned", "ab3")
        for c in range(CH):
            nc.tensor.transpose(turned[:, c * P : (c + 1) * P], wgs_rows[:, c * P : (c + 1) * P], ident[:])
        spread = sbuf("spread", [CH, PACK, PACK, QUAD], F32, "AA")
        for c in range(CH):
            rows = turned[:, c * P : (c + 1) * P].rearrange("p (q t) -> p t q", t=PACK)
            nc.scalar.copy(spread[:, c], rows.unsqueeze(2).to_broadcast([P, PACK, PACK, QUAD]))
        wgs_dealt = sbuf("wgs_dealt", [PACK, S], F32)
        for t, which in enumerate(("hh3", "hh2", "ab2", "hh1")):
            acc = bank("wgs_back%d" % t, which)
            for c in range(CH):
                nc.tensor.transpose(acc[:, c * P : (c + 1) * P], spread[:, c, t].rearrange("p r q -> p (r q)"), ident[:])
            nc.scalar.copy(wgs_dealt[:, t, :], acc[:])
            factors.append(wgs_dealt[:, t, :])

        def put(s, h):
            nc.vector.tensor_tensor(pages[s][:].indirect(idx2[:]), h[:], factors[s], MULT)

        def plain_weights(name, rows, copies, buffer, last_buffer):
            width = rows[0].shape[2] * PACK
            first = sbuf(name + "_woven", [KP - 1, width], BF16, buffer)
            quantised = []
            for a in range(KP):
                woven = first[:, a] if a < KP - 1 else sbuf(name + "_last", [width], BF16, last_buffer)[:]
                quantised.append(quantize("%s_q%d" % (name, a), weave(copies[a], woven, rows[a])))
            return quantised

        def plain_abs(s):
            acc = bank("b%d" % s, "hh%d" % s)
            words, first = (w2_first, 0) if s == 0 else (w2_rest, (s - 1) * P)
            for a in range(KP):
                nc.tensor.matmul_mx(
                    out=acc[:], lhsT=words[:, a, 2 * first : 2 * (first + P)].bitcast(FP4X4),
                    lhsT_scale=w2_plane_plain[:, a, s * P : (s + 1) * P],
                    rhs=vw[a][:].bitcast(FP8X4), rhs_scale=vs[a][:], start=(a == 0), stop=(a == KP - 1),
                )
            mag = sbuf("mag%d" % s, [S], F32, "h%d" % s)
            nc.scalar.activation(mag[:], acc[:], ACT.Abs)
            return mag

        def plain_linear(s, which, quantised, first):
            acc = bank("a%d" % s, which)
            for a in range(KP):
                codes, scales = quantised[a]
                nc.tensor.matmul_mx(
                    out=acc[:], lhsT=codes[:, first : first + P].bitcast(FP8X4), lhsT_scale=scales[:, first : first + P],
                    rhs=vw[a][:].bitcast(FP8X4), rhs_scale=vs[a][:], start=(a == 0), stop=(a == KP - 1),
                )
            return acc

        def plain_put(s, acc, mag, buffer):
            nc.vector.tensor_tensor(mag[:], acc[:], mag[:], ADD)
            put(s, mag)
            recalled = sbuf("x_plain%d" % s, [S], F32, buffer)
            nc.vector.tensor_copy(recalled[:], pages[s][:].indirect(idx3[:]))
            return recalled

        q0 = plain_weights("w1_0", w1_0, (nc.scalar.copy, nc.vector.tensor_copy, nc.vector.tensor_copy), "H0", "W0")
        mags = [plain_abs(0)]
        acc = plain_linear(0, "ab0", q0, 0)
        q1 = plain_weights("w1_1", w1_1, [nc.scalar.copy] * KP, "H1", "W1")
        x_plain = [plain_put(0, acc, mags[0], "W1")]
        mags.extend(plain_abs(s) for s in range(1, PACK))
        acc = plain_linear(1, "ab1", q1, 0)
        q23 = plain_weights("w1_23", w1_23, [nc.scalar.copy] * KP, "H0", "W2")
        x_plain.append(plain_put(1, acc, mags[1], "W2"))
        acc = plain_linear(2, "ab2", q23, 0)
        x_plain.append(plain_put(2, acc, mags[2], "W0"))
        acc = plain_linear(3, "ab2", q23, P)

        for s in range(PACK - 1, 2 * PACK):
            pages[s] = load_page(s)
        w3_rows = [load_rows(sbuf("w3_rows0", [PACK, H], F32, "R3")[:], w3, 0, 0)]

        def add_turned(acc, src, t, c, start, stop):
            nc.tensor.matmul(acc[:, c * P : (c + 1) * P], src[:, c, t, :], ident[:], start=start, stop=stop, is_transpose=True)

        pair = sbuf("w1_dealt_woven", [2, BLOCK * PACK], BF16, "AA")
        woven = [weave(nc.scalar.copy, pair[:, a], w1_dealt[a]) for a in range(2)]
        last = sbuf("w1_dealt_last", [2, HALF * PACK], BF16, "AB")
        for u, copy in enumerate((nc.scalar.copy, nc.vector.tensor_copy)):
            weave(copy, last[:, u], w1_dealt[2][:, :, u * HALF : (u + 1) * HALF])
        woven.append(last[:].rearrange("p u c -> p (u c)"))
        mag_turned = sbuf("mag_turned", [CH, PACK, P], F32, "R2")
        for c in range(CH):
            b_turned = bank("b_turned%d" % c, "hh%d" % c)
            cols = slice(c * P, (c + 1) * P)
            for a in range(KP):
                nc.tensor.matmul_mx(
                    out=b_turned[:], lhsT=vw[a][:, cols].bitcast(FP8X4), lhsT_scale=vs[a][:, cols],
                    rhs=w2_dealt[:, a, :].bitcast(FP4X4), rhs_scale=w2_plane_dealt[:, a, :],
                    start=(a == 0), stop=(a == KP - 1),
                )
            nc.scalar.activation(mag_turned[:, c], by_slice(b_turned), ACT.Abs)
        a_turned = [bank("a_turned%d" % c, "ab%d" % ((c + 3) % CH)) for c in range(CH)]
        q_dealt = [quantize("w1_dealt_q%d" % a, woven[a]) for a in range(KP)]
        x_plain.append(plain_put(3, acc, mags[3], "W3"))
        sums = [bank("sum%d" % t, "hh%d" % t) for t in range(PACK)]
        for c in range(CH):
            add_turned(sums[0], mag_turned, 0, c, c == 0, False)
        for a in range(KP):
            codes, scales = q_dealt[a]
            for c in range(CH):
                cols = slice(c * P, (c + 1) * P)
                nc.tensor.matmul_mx(
                    out=a_turned[c][:], lhsT=vw[a][:, cols].bitcast(FP8X4), lhsT_scale=vs[a][:, cols],
                    rhs=codes[:].bitcast(FP8X4), rhs_scale=scales[:], start=(a == 0), stop=(a == KP - 1),
                )

        x0 = sbuf("x0", [PACK, S], F32, "R1")
        x = {(0, 0): x0[:, :, :HALF], (0, 1): x0[:, :, HALF:]}
        w3_rows.append(load_rows(sbuf("w3_rows1", [PACK, H], F32, "R4")[:], w3, 1, 0))
        for t in range(PACK):
            for s in (0, 2, 1, 3):
                nc.sync.dma_start(out=x0[QUAD * s : QUAD * (s + 1), t, :], in_=x_plain[s][t:P:PACK, :])

        g2 = sbuf("g2", [HB, PACK], F32)
        load(g2[:], gain2.rearrange("(b p t) -> p b t", b=HB, t=PACK))
        idx4 = load_list("idx4", offs4)
        w4_plane = load_scales("w4_plane", w4_scales, HB, N)
        w4w = sbuf("w4w", [HB, N], I32)
        load(w4w[:], w4_words.rearrange("a p n t -> p a (n t)").bitcast(I32))
        wo = sbuf("wo", [S], F32)
        load(wo[:], wgo)
        walk = []
        for n, buffer in enumerate((None, None, None, "R3", "R0")):
            walk.append(sbuf("walk%d" % n, [T2], F32, buffer))
            load(walk[n][:], page1[n * P : (n + 1) * P, :])

        def state(t, buffer):
            h = sbuf("h_dealt%d" % t, [S], F32, buffer)
            nc.scalar.activation(h[:], sums[t][:], ACT.Copy, scale=g1_dealt[:, t : t + 1])
            return h

        def recall(t, half):
            window = pages[PACK + t][:].indirect(idx3[:, half * LCOL : (half + 1) * LCOL])
            nc.vector.tensor_copy(x[1, half][:, t, :], window)

        lin_first = sbuf("lin_first", [CH, 1, P], F32, "AA")
        for c in range(CH):
            nc.scalar.copy(lin_first[:, c, 0], by_slice(a_turned[c])[:, 0])
        for c in range(CH):
            add_turned(sums[0], lin_first, 0, c, False, c == CH - 1)
        hs = [state(0, "h4")]
        lin = sbuf("lin", [CH, PACK, P], F32, "AA")
        for c in range(CH):
            nc.scalar.copy(lin[:, c, 1:], by_slice(a_turned[c])[:, 1:])
        for t in range(1, PACK):
            for c in range(CH):
                add_turned(sums[t], lin, t, c, c == 0, False)
                add_turned(sums[t], mag_turned, t, c, False, c == CH - 1)
        hs.extend(state(t, buffer) for t, buffer in ((1, "h5"), (2, "h0"), (3, "h1")))

        x[1, 0] = sbuf("x10", [PACK, HALF], F32, "H1")[:]
        put(PACK, hs[0])
        recall(0, 0)
        pair = sbuf("w3_woven", [HB, BLOCK * PACK], BF16, "AA")
        w3_woven = {(a, 0): weave_dealt(pair[:, a], w3_rows[a][:, :, :BLOCK]) for a in range(HB)}
        put(PACK + 1, hs[1])
        for a, buffer in enumerate(("H0", "AB")):
            w3_woven[a, 1] = weave_dealt(sbuf("w3_woven%d1" % a, [BLOCK * PACK], BF16, buffer)[:], w3_rows[a][:, :, BLOCK:])
        x00_woven = weave(nc.scalar.copy, sbuf("x00_woven", [HALF * PACK], BF16, "h5")[:], x[0, 0])
        for t in range(2, PACK):
            put(PACK + t, hs[t])
            recall(t - 1, 0)
        recall(PACK - 1, 0)
        x10_woven = weave(nc.scalar.copy, sbuf("x10_woven", [HALF * PACK], BF16, "W3")[:], x[1, 0])
        planes = sbuf("planes_first", [2, BLOCK], U8, "h1")
        w3q = {(0, 0): quantize("w3q00", w3_woven[0, 0], planes[:, 0])}
        xq = {(0, 0): quantize("xq00", x00_woven, planes[:, 1, :HALF])}
        planes = sbuf("planes_rest", [3, BLOCK], U8, "h5")
        w3q[1, 0] = quantize("w3q10", w3_woven[1, 0], planes[:, 2])
        xq[1, 0] = quantize("xq10", x10_woven)
        for a in range(HB):
            w3q[a, 1] = quantize("w3q%d1" % a, w3_woven[a, 1], planes[:, a])

        def features(half):
            accs = [bank("e%d%d" % (half, k), "ab%d" % k) for k in range(4)]
            for a in range(HB):
                for k in range(4):
                    b, first = k // 2, 2 * (k % 2)
                    for u in range(2):
                        cols = slice((first + u) * P, (first + u + 1) * P)
                        nc.tensor.matmul_mx(
                            out=accs[k][:, u * HALF : (u + 1) * HALF],
                            lhsT=w3q[a, b][0][:, cols].bitcast(FP8X4), lhsT_scale=w3q[a, b][1][:, cols],
                            rhs=xq[a, half][0][:].bitcast(FP8X4), rhs_scale=xq[a, half][1][:],
                            start=(a == 0 and u == 0), stop=(a == HB - 1 and u == 1),
                        )
            tanhs = []
            for k in range(4):
                tanhs.append(sbuf("tanh%d%d" % (half, k), [2, HALF], F32, "B%d" % k))
                nc.scalar.activation(tanhs[k][:].rearrange("p u j -> p (u j)"), accs[k][:], ACT.Tanh)
            return tanhs

        def combine(half, k, tanhs, z):
            b, first = k // 2, 2 * (k % 2)
            for u in range(2):
                t = first + u
                nc.vector.scalar_tensor_tensor(z[:, t, :], tanhs[k][:, u, :], g2[:, b, t : t + 1], x[b, half][:, t, :], MULT, ADD)

        def woven_tile(name, buffer):
            return sbuf(name, [HALF * PACK], BF16, buffer)[:]

        zq = {}

        def last_product(half, n, which):
            acc = bank("y%d%d" % (half, n), which)
            cols = slice(n * P, (n + 1) * P)
            for a in range(HB):
                nc.tensor.matmul_mx(
                    out=acc[:, :HALF], lhsT=w4w[:, a, cols].bitcast(FP8X4), lhsT_scale=w4_plane[:, a, cols],
                    rhs=zq[a, half][0][:].bitcast(FP8X4), rhs_scale=zq[a, half][1][:],
                    start=(a == 0), stop=(a == HB - 1),
                )
            return acc

        def leave(half, n, acc, buffer):
            y = sbuf("y_out%d%d" % (half, n), [HALF], F32, buffer)
            nc.scalar.copy(y[:], acc[:, :HALF])
            return y

        def place(half, n, y):
            window = walk[n][:].indirect(idx4[:, half * LCOL : (half + 1) * LCOL])
            nc.vector.tensor_tensor(window, y[:], wo[:, half * HALF : (half + 1) * HALF], MULT)

        tanhs = features(0)
        z0 = sbuf("z00", [PACK, HALF], BF16, "h2")
        z1 = sbuf("z10", [PACK, HALF], BF16, "h3")
        combine(0, 0, tanhs, z0)
        combine(0, 1, tanhs, z0)
        z0_woven = weave(nc.scalar.copy, woven_tile("z00_woven", "h4"), z0[:])
        combine(0, 2, tanhs, z1)
        combine(0, 3, tanhs, z1)
        x11 = sbuf("x11", [PACK * HALF], F32, "H1")
        x[1, 1] = x11[:].rearrange("p (t j) -> p t j", t=PACK)
        z1_woven = weave(nc.scalar.copy, x11[:, 2 * HALF :].bitcast(BF16), z1[:])
        zq[0, 0] = quantize("zq00", z0_woven)
        recall(0, 1)
        recall(1, 1)
        zq[1, 0] = quantize("zq10", z1_woven)
        recall(2, 1)
        recall(3, 1)
        xq[0, 1] = quantize("xq01", weave(nc.scalar.copy, woven_tile("x01_woven", "h3"), x[0, 1]))
        ys = [last_product(0, n, "hh%d" % n) for n in range(NT - 1)]
        place(0, 0, leave(0, 0, ys[0], "G0"))
        ys.append(last_product(0, NT - 1, "hh0"))
        place(0, 1, leave(0, 1, ys[1], "G1"))
        xq[1, 1] = quantize("xq11", weave(nc.scalar.copy, woven_tile("x11_woven", "h0"), x[1, 1]))
        place(0, 2, leave(0, 2, ys[2], "G2"))

        tanhs = features(1)
        z0 = sbuf("z01", [PACK, HALF], BF16, "h1")
        z1 = sbuf("z11", [PACK, HALF], BF16, "h2")
        combine(1, 0, tanhs, z0)
        combine(1, 1, tanhs, z0)
        combine(1, 2, tanhs, z1)
        y3 = leave(0, 3, ys[3], "B2")
        combine(1, 3, tanhs, z1)
        z0_woven = weave(nc.scalar.copy, woven_tile("z01_woven", "h4"), z0[:])
        z1_woven = weave(nc.scalar.copy, woven_tile("z11_woven", "h5"), z1[:])
        place(0, 3, y3)
        zq[0, 1] = quantize("zq01", z0_woven)
        zq[1, 1] = quantize("zq11", z1_woven)
        place(0, 4, leave(0, 4, ys[4], "h2"))
        for n, buffer in enumerate(("G0", "G1", "G2", "B0", "B1")):
            place(1, n, leave(1, n, last_product(1, n, "hh%d" % ((n + 1) % 4)), buffer))
            nc.sync.dma_start(out=out[n * P : (n + 1) * P, :], in_=walk[n][:])
